import numpy as np, ml_dtypes
CORES = [10,34,74,98]
N = 4
BF = ml_dtypes.bfloat16
V, W, P, CAP, RO = 1024, 4096, 2, 64, 3
def mates(rng):
    o = np.argsort(rng.random((8, 16, W)), axis=-1); m = np.zeros((8, 16, W), np.int64)
    np.put_along_axis(m, o[..., 0::2], o[..., 1::2], -1); np.put_along_axis(m, o[..., 1::2], o[..., 0::2], -1)
    return m, o
def cliques(rng, s, who):
    i = 0
    while i < len(who):
        m = int(rng.integers(2, 10)); c = who[i:i + m]; m = len(c); i += m
        if m > 1: s[np.argsort(rng.random((m, 16)), axis=1)[:, :m - 1], c[:, None]] = c[(np.arange(m)[:, None] + 1 + np.arange(m - 1)) % m]
def net(rng):
    m, o = mates(rng); keep = rng.choice(np.array([0.0, 0.1, 0.25, 0.4, 0.6, 1.0]), (8, 1, W))
    s = np.where(rng.random(m.shape) < keep, m, W); twins = []
    for g in range(8):
        i = rng.permutation(W // 2)[:W // 16]; v = o[g, 0, 2 * i]; b = o[g, 0, 2 * i + 1]
        s[g][:, b] = m[g][:, b]; s[g][0, b] = rng.integers(0, W, len(b)); s[g][0, v] = b
        who = rng.permutation(np.setdiff1d(np.arange(W), np.concatenate([v, b])))[:W // 8]
        s[g][:, who] = W; cliques(rng, s[g], who); twins.append((v, b))
    return s, twins
def pack(x, s):
    cut = lambda a: np.ascontiguousarray(a.reshape(8, 16, N, V).transpose(2, 0, 1, 3).reshape(N, 128, V))
    return {"x": cut(x).astype(np.float32).astype(BF), "stars": cut(s).astype(np.int32)}
def same(x, twins):
    for g in range(8): x[g][:, twins[g][0]] = x[g][:, twins[g][1]]
    return x
def setup_inputs(rng):
    s, twins = net(rng)
    return pack(same(rng.integers(0, 256, (8, 16, W)), twins), s)
def full(rng, s, x):
    a = int(rng.integers(0, N)); v = np.concatenate([q * V + rng.permutation(np.arange(0, V, P))[:CAP] for q in range(N)])
    b = rng.permutation(np.setdiff1d(np.arange(a * V, (a + 1) * V), v))[:N * CAP]
    s[0, v] = b; s[10, v] = rng.choice(np.setdiff1d(np.arange(W), np.concatenate([v, b])), len(v))
def far(rng, s, x):
    o = rng.permutation(W); v = o[o % P == 0][:CAP]; rest = o[~np.isin(o, v)]; b = rest[:CAP]; e = rest[CAP:2 * CAP]; i = np.arange(CAP) & 3
    low = rng.integers(1, 16, (16, CAP)); high = rng.integers(240, 253, (16, CAP))
    high[0] += (np.where(i == 2, 3, 1) - np.add.reduce(high - low, axis=0)) & 3
    near = low.copy(); near[1] += 1; near[2] -= (i == 2).astype(np.int64)
    x[:, b] = low; x[:, v] = np.where(i == 3, near, high); x[:, e] = np.where(i == 3, high, near)
    s[rng.integers(0, 16, CAP), v] = b; m = i > 0; s[8, b[m]] = e[m]; s[0, e[m]] = b[m]
    cliques(rng, s, rest[2 * CAP:])
def again(rng, s, x):
    ends = np.array([0, V - 2, V - 1]); o = [q * V + rng.permutation(np.arange(1, V - 2)) for q in range(N)]
    v = [a[a % P == 0][:CAP] for a in o]; rest = [a[~np.isin(a, c)] for a, c in zip(o, v)]
    for q in range(N):
        b = rest[(q + 1) % N][:CAP]; s[rng.integers(0, 16, CAP), v[q]] = b; x[:, b] = x[:, v[q]]
        s[rng.integers(0, 16, 3), q * V + ends] = rest[(q + 2) % N][CAP:CAP + 3]
        cliques(rng, s, rest[q][CAP + 3:])
def setup_inputs_room(rng):
    s = np.full((8, 16, W), W, np.int64); cyc = (CAP, CAP + 1, CAP - 1, 1, 0); rows = np.arange(16)[:, None]
    x = rng.integers(0, 256, (8, 16, W)); kind = rng.permutation(8)
    for g in range(8):
        if kind[g] > 4:
            (full, far, again)[int(kind[g]) - 5](rng, s[g], x[g])
            continue
        talk = np.zeros(W, bool); to = []
        for q in range(N):
            act = rng.permutation(np.arange(0, V, P)); left = 3 * len(act) // 4; pos = 0
            for d in [0] + list(range(1, N)):
                n = min(cyc[(d - 1 + int(kind[g])) % 5], left - pos); v = q * V + act[pos:pos + n]; pos += n
                talk[v] = True; to.append((v, (q + d) % N))
        rest = rng.permutation(np.flatnonzero(~talk)); cliques(rng, s[g], rest)
        for v, a in to:
            n = len(v); b = rng.choice(rest[rest // V == a], n); k = rng.integers(0, 16, n)
            s[g][:, v] = np.where(rows == k, b, np.where((rows > k) & (rng.random((16, n)) < 0.4), rng.integers(0, W, (16, n)), W))
    return pack(x, s)
def setup_inputs_ties(rng):
    m, o = mates(rng); s = np.where(rng.random(m.shape) < rng.choice(np.array([0.1, 0.4, 0.9, 1.0]), (8, 1, W)), m, W)
    n = rng.permutation(np.array([1, 1, 2, 2, 2, 3, 3, 4]))[:, None, None]
    x = rng.integers(0, 252, (8, 16, 1)) + (rng.random((8, 16, W)) * n).astype(np.int64)
    return pack(x, s)
def setup_inputs_alike(rng):
    s, o = mates(rng); kind = rng.permutation(8) & 3
    for g in range(8):
        q = int(rng.integers(0, N))
        if kind[g] == 0: s[g] = rng.choice(np.array([0, V - 1, V, W - 1]), (16, W))
        elif kind[g] == 1: s[g] = rng.integers(q * V, (q + 1) * V, (16, W))
        elif kind[g] == 2: s[g, 1::2] = s[g, 0::2]; s[g, 4] = np.arange(W)
        else: s[g] = np.repeat(s[g, :1], 16, axis=0); s[g][:, q * V:(q + 1) * V] = W
    s = np.where(rng.random(s.shape) < rng.choice(np.array([0.3, 0.6, 0.9]), (8, 1, W)), s, W)
    return pack(rng.integers(0, 256, (8, 16, W)), s)
def setup_inputs_line(rng):
    m, o = mates(rng); s = np.where(rng.random(m.shape) < rng.choice(np.array([0.3, 0.7, 1.0]), (8, 1, W)), m, W)
    p = rng.integers(0, 256, (8, 1, W)); x = np.where(rng.random((8, 16, 1)) < 0.5, p, 255 - p)
    for g in range(8):
        i = np.argsort(p[g, 0] + rng.random(W)).reshape(-1, 64); low = i[:, :32].reshape(-1); high = i[:, 32:].reshape(-1)
        up = rng.random(len(low)) < 0.5; v = np.where(up, low, high); b = np.where(up, high, low)
        s[g, 0, v] = b; s[g, 0, b] = rng.integers(0, W, len(b))
    return pack(x, s)
def setup_inputs_spread(rng):
    s, twins = net(rng)
    x = (np.exp2(8 * rng.random((8, 1, W))) * rng.random((8, 16, W)) * (rng.random((8, 1, W)) > 0.0625)).astype(np.int64)
    return pack(same(np.minimum(x, 255), twins), s)
def check_inputs(d):
    bad = []; v = np.asarray(d["x"]).astype(np.float32)
    if not (np.min(v) >= 0 and np.max(v) <= 255 and np.all(v == np.floor(v))): bad.append("x: whole numbers from 0 to 255")
    if np.min(d["stars"]) < 0 or np.max(d["stars"]) > W: bad.append("range of stars")
    return bad
def judge(pts, e, b, z):
    live = e < W; xz = pts[z]; xb = pts[b]; xe = pts[e]
    ez = np.add.reduce(np.abs(xe - xz[:, None, :]), axis=2); eb = np.add.reduce(np.abs(xe - xb[:, None, :]), axis=2)
    zb = np.add.reduce(np.abs(xz - xb), axis=1)
    block = np.any(live & (ez < zb[:, None]), axis=1)
    new = np.where(live & (ez < eb), W, e); free = new == W
    new[np.arange(len(b)), np.argmax(free, axis=1)] = z
    return np.where((~block & np.any(free, axis=1))[:, None], new, e)
def reference(x, stars):
    pts = np.zeros((8, W + 1, 16), np.int64); st = np.full((8, W + 1, 16), W, np.int64)
    pts[:, :W] = x.astype(np.float32).astype(np.int64).reshape(N, 8, 16, V).transpose(1, 0, 3, 2).reshape(8, W, 16)
    st[:, :W] = stars.astype(np.int64).reshape(N, 8, 16, V).transpose(1, 0, 3, 2).reshape(8, W, 16)
    for t in range(RO):
        act = np.flatnonzero((np.arange(W) % V) % P == t % P); src = act // V; ks = (5 * t + np.arange(16)) & 15
        new = st.copy()
        for g in range(8):
            mine = st[g][act]; b = mine[:, ks]; c = mine[:, (ks + 1) & 15]; sb = st[g][b]
            hasv = np.any(sb == act[:, None, None], axis=2); hasc = np.any(sb == c[:, :, None], axis=2)
            one = (b < W) & ~hasv; two = (b < W) & hasv & (c < W) & ~hasc
            some = np.any(one | two, axis=1); j = np.argmax(one | two, axis=1); i = np.arange(len(act))
            to = b[i, j]; z = np.where(one[i, j], act, c[i, j])
            for a in range(N):
                here = some & (to // V == a)
                ix = np.concatenate([np.flatnonzero(here & (src == q))[:CAP] for q in range(N)])
                ix = ix[np.unique(to[ix], return_index=True)[1]]
                new[g, to[ix]] = judge(pts[g], st[g][to[ix]], to[ix], z[ix])
        st = new
    y = st[:, :W].reshape(8, N, V, 16).transpose(1, 0, 3, 2).reshape(N, 128, V)
    return {"y": np.ascontiguousarray(y).astype(np.float32)}

@@ -1,0 +1,569 @@
+import numpy as np
+from concourse.bass import DstId, RemoteDMATransfer
+from concourse.mybir import AluOpType as OP, ActivationFunctionType as AF
+
+N, V, W, RO = 4, 1024, 4096, 3
+SH = 2048.0
+BIG = 8192.0
+TW = W + 8 + 256
+C0 = 520
+HC = 384
+CH = [32, 32] + [64] * 7
+PCH = [128, 128, 128, 128]
+BOOST, DB, LOOK, TRIES = 30000.0, 5000.0, 100.0, 1200
+CYC, PEC, GA, SC, HOP = 1.04, 0.52, 1.56, 3.8, 120.0
+FIGS = ((1.0, 1.56, 120.0), (0.85, 1.15, 200.0), (1.15, 2.0, 70.0))
+MATS = ["I", "NI", "IB", "NIB", "ISH", "BDH", "NBDH", "BDB", "NBDB", "I4", "TR0", "TR1", "TR2", "BD", "S1", "S2", "NBD"]
+F, B, H16, U16, I32 = "float32", "bfloat16", "float16", "uint16", "int32"
+SCRATCH = {n: ("sbuf", [128, w], d) for n, w, d in [
+    ("sti", V, I32), ("lan", W, H16), ("tab", TW, F), ("xt", W + 16, B), ("gg", 8192, F), ("e1", 8192, B), ("e2", 8192, B),
+    ("xe", 4096, B), ("mb", 128 * len(MATS), B), ("sel", 2048, H16), ("mf", 256, H16), ("l32", 384, F), ("zb", 432, B),
+    ("zf", 432, H16), ("ones", 256, B), ("mhalf", 128, B), ("cc", 16, F), ("ci", 4, I32), ("om", 384, I32), ("wf", 512, F),
+    ("w16", 1024, H16), ("dw", 16, F), ("s16", 512, H16), ("so", 512, U16), ("non", 512, B), ("sg", 1536, B), ("ao", 1024, B),
+    ("b16", 16, B), ("rr", 1536, F), ("bzs", 512, F), ("ab", 512, F), ("ind", 512, H16), ("val", 512, F), ("prod", 512, H16),
+    ("co", 32, U16), ("cb", 2576, F), ("c16", 320, H16), ("obz", 32, U16), ("eo", 256, U16), ("xbz", 512, B), ("sbf", 256, F),
+    ("nj", 256, B), ("dzb", 256, B), ("fl", 512, B), ("er", 512, B), ("uu", 256, F), ("bbs", 256, F), ("inv", 256, B),
+    ("eq", 1024, B), ("cnt", 256, B), ("tg", 16, F), ("md", RO * 1024, H16), ("mo", RO * 64, U16), ("yb", V, F)]}
+for _i in range(8):
+    SCRATCH["p%d" % _i] = ("psum", [128, 512], F)
+SEMAPHORES = ["qv", "qa", "qp", "qg", "ld0", "ld1", "ldx", "st0", "st1", "loc", "hin"]
+for _s in range(N):
+    SEMAPHORES += ["sa%d" % _s, "sb%d" % _s, "sh%d" % _s, "sx%d" % _s]
+    for _t in range(RO):
+        SEMAPHORES += ["mo%d%d" % (_t, _s), "md%d0%d" % (_t, _s), "md%d1%d" % (_t, _s)]
+
+
+def helper_of(c, peers, topo):
+    return [h for h in topo.cores_of(c) if topo.die(h) != topo.die(c) and all(topo.may_write(h, p) for p in peers)][0]
+
+
+def transfer(topo, dst_cores, ap, sem, engines):
+    ids = [DstId(rid=topo.addr(d)[0], pnc=topo.addr(d)[1]) for d in dst_cores]
+    return RemoteDMATransfer(dst_ids=ids, dma_engine_mask=sum(1 << e for e in engines), remote_sem=sem, srcs=[ap], dsts=[ap] * len(ids))
+
+
+def common_engines(src, dsts, topo):
+    return [e for e in topo.engines(src, dsts[0]) if all(e in topo.engines(src, d) for d in dsts)]
+
+
+def R(name, lo, hi, st=1, rows=128):
+    return (name, lo, hi, st, rows)
+
+
+def width(r):
+    return len(range(r[1], r[2], r[3]))
+
+
+def bits(r):
+    return (((1 << (width(r) * r[3])) - 1) // ((1 << r[3]) - 1)) << r[1]
+
+
+def build(g, core, T, topo):
+    rank = T.rank_of(core)
+    peers = [c for c in T.cores if c != core]
+    others = [s for s in range(N) if s != rank]
+    off_eng = common_engines(core, peers, topo)
+    NE = len(off_eng)
+    ops, acc, nloc, boost, base = [], {}, [0], [0.0], [-1000]
+    Q = {"v": g.vector, "a": g.scalar, "p": g.tensor, "g": g, "s": g.sync}
+
+    def ap(r):
+        return T[r[0]][0:r[4], r[1]:r[2]:r[3]] if r[3] != 1 else T[r[0]][0:r[4], r[1]:r[2]]
+
+    def add(eng, fn, cost, rd=(), wr=(), after=(), sem=None, val=0, lat=0.0, ga=0):
+        i = len(ops)
+        deps = {}
+        for r, w in [(r, False) for r in rd] + [(r, True) for r in wr]:
+            ps = SCRATCH[r[0]][0] == "psum"
+            m = bits(r)
+            keep = []
+            for (j, mj, wj) in acc.get(r[0], []):
+                if j == i:
+                    keep.append((j, mj, wj))
+                    continue
+                same = ops[j]["eng"] == eng and ops[j]["sem"] is None and sem is None
+                hit = bool(m & mj) and (w or wj)
+                if ps and (not same or eng == "p"):
+                    hit = True
+                if hit:
+                    deps[j] = deps.get(j, False) or not (same and eng == "p")
+                if not (w and (mj & ~m) == 0 and hit):
+                    keep.append((j, mj, wj))
+            keep.append((i, m, w))
+            acc[r[0]] = keep
+        for j in after:
+            deps[j] = deps.get(j, False)
+        ops.append({"eng": eng, "fn": fn, "cost": cost, "deps": deps, "sem": sem, "val": val, "lat": lat, "boost": boost[0],
+                    "tag": i - base[0], "ga": ga, "pe": eng == "p"})
+        return i
+
+    def sc(x):
+        return ap(x) if isinstance(x, tuple) else x
+
+    def src(x):
+        if x[0] == "ind":
+            return ap(x[1]).indirect(ap(x[2])), [x[1], x[2]], GA
+        return ap(x), [x], 1.0
+
+    def two(*rs):
+        return all(SCRATCH[r[0]][2] in (B, H16, U16) for r in rs)
+
+    def ts(out, in0, s1, s2, o0, o1=None, after=()):
+        a, rd, f = src(in0)
+        if f == 1.0 and two(out, in0):
+            f = 0.5
+        rd = rd + [s for s in (s1, s2) if isinstance(s, tuple)]
+        if o1 is None:
+            fn = lambda: g.vector.tensor_scalar(ap(out), a, sc(s1), None, o0)
+        else:
+            fn = lambda: g.vector.tensor_scalar(ap(out), a, sc(s1), sc(s2), o0, o1)
+        return add("v", fn, 60 + CYC * max(64, f * width(out)), rd, [out], after)
+
+    def tt(out, a, b, o, after=()):
+        f = 1 if SCRATCH[b[0]][0] == "psum" else 2
+        return add("v", lambda: g.vector.tensor_tensor(ap(out), ap(a), ap(b), o), 60 + CYC * max(64, f * width(out)), [a, b], [out], after)
+
+    def cp(out, in_, after=()):
+        a, rd, f = src(in_)
+        if f == 1.0 and two(out, in_):
+            f = 0.5
+        return add("v", lambda: g.vector.tensor_copy(ap(out), a), 60 + CYC * max(64, f * width(out)), rd, [out], after)
+
+    def scat(win, off, a, after=()):
+        return add("v", lambda: g.vector.tensor_copy(ap(win).indirect(ap(off)), ap(a)), 60 + CYC * SC * width(a), [off, a], [win], after)
+
+    def ms(out, c):
+        return add("v", lambda: g.vector.memset(ap(out), c), 60 + CYC * max(64, width(out)), [], [out])
+
+    def scan(out, d0, d1, init, o0, o1):
+        rd = [d0, d1] + ([init] if isinstance(init, tuple) else [])
+        return add("v", lambda: g.vector.tensor_tensor_scan(ap(out), ap(d0), ap(d1), sc(init), o0, o1), 60 + CYC * max(64, width(out)), rd, [out])
+
+    def act(out, in_, func, bias=0.0, after=()):
+        a, rd, f = src(in_)
+        rd = rd + ([bias] if isinstance(bias, tuple) else [])
+        return add("a", lambda: g.scalar.activation(ap(out), a, func, bias=sc(bias)), 80 + CYC * max(64, f * width(out)), rd, [out], after,
+                   ga=width(out) if f == GA else 0)
+
+    def mm(terms, start=True, stop=True):
+        def fn():
+            for n, (o, l, r) in enumerate(terms):
+                ins = g.tensor.matmul(ap(o), ap(l), ap(r), start and n == 0, stop and n == len(terms) - 1)
+            return ins
+        cost = 30 + sum(PEC * max(64, width(r)) * (4 if SCRATCH[r[0]][2] == F else 1) for (o, l, r) in terms)
+        return add("p", fn, cost, list(set([l for (o, l, r) in terms] + [r for (o, l, r) in terms])), list(set(o for (o, l, r) in terms)))
+
+    def iota(out, pat, start, cm, after=()):
+        if SCRATCH[out[0]][2] == I32:
+            fn = lambda: g.iota(ap(out), pat, start, cm)
+        else:
+            fn = lambda: g.iota(ap(out), pat, start, cm, allow_small_or_imprecise_dtypes=True)
+        return add("g", fn, 150 + 2 * CYC * width(out), [], [out], after)
+
+    def asel(out, a, pat, cmp, fill, start, cm, after=()):
+        return add("g", lambda: g.affine_select(ap(out), ap(a), pat, cmp, fill, start, cm), 200 + 2 * CYC * width(out), [a], [out], after)
+
+    def send(parts, sem, engines, after=()):
+        k = len(engines) // len(parts)
+        nloc[0] += k * len(parts)
+        fn = lambda: g.remote_dma_fused([transfer(topo, d, ap(r), T.sem[sem], engines[k * n:k * n + k]) for n, (r, d) in enumerate(parts)],
+                                        local_sem=T.sem.loc)
+        return add("g", fn, 700, [r for r, d in parts], [], after, lat=-1.0)
+
+    def arrive(r, sem, val, after, lat):
+        return add("x", None, 0, [], [r], after, sem=sem, val=val, lat=lat)
+
+    def M(name):
+        k = MATS.index(name)
+        return R("mb", 128 * k, 128 * k + 128)
+
+    def g8(name):
+        return R("mb", M(name)[1], M(name)[2], 16)
+
+    def Z(buf, n, k):
+        return R(buf, 144 * n + 15 - k, 144 * n + 143 - k)
+
+    def SEL(k):
+        return R("sel", 128 * k, 128 * k + 128)
+
+    def col(k):
+        return R("cc", k, k + 1)
+
+    me = V * rank
+    DC = V - HC
+    D2 = DC // 2
+    IF, SHF = R("mf", 0, 128), R("mf", 128, 256)
+    LB, LZ = R("l32", 0, 128), R("l32", 128, 256)
+    boost[0] = BOOST
+    add("s", lambda: g.sync.dma_start(T.sti[:, DC:V], T.stars[:, DC:V]), 50, [], [R("sti", DC, V)], sem="ld0", val=16, lat=2600)
+    add("a", lambda: g.scalar.dma_start(T.sti[:, 0:DC], T.stars[:, 0:DC]), 50, [], [R("sti", 0, DC)], sem="ld1", val=16, lat=3200)
+    add("s", lambda: g.sync.dma_start(T.xt[:, me:me + V], T.x[:, :]), 50, [], [R("xt", me, me + V)], sem="ldx", val=16, lat=4000)
+    hp = helper_of(core, peers, topo)
+    ts(R("lan", me + DC, me + V), R("sti", DC, V), -SH, None, OP.add)
+    s_h = send([(R("lan", me + DC, me + V), [hp])], "hin", [e for e in topo.engines(core, hp) if e not in off_eng])
+    ts(R("lan", me, me + D2), R("sti", 0, D2), -SH, None, OP.add)
+    s_a = send([(R("lan", me, me + D2), peers)], "sa%d" % rank, off_eng, [s_h])
+    ts(R("lan", me + D2, me + DC), R("sti", D2, DC), -SH, None, OP.add)
+    s_b = send([(R("lan", me + D2, me + DC), peers)], "sb%d" % rank, off_eng, [s_a])
+    s_x = send([(R("xt", me, me + V), peers)], "sx%d" % rank, off_eng, [s_b])
+    boost[0] = 0.0
+
+    ms(R("ones", 0, 256), 1.0)
+    ms(R("mhalf", 0, 128), -0.5)
+    ms(R("zb", 0, 432), 0.0)
+    ts(R("zf", 0, 432), R("zb", 0, 432), 0.0, None, OP.mult)
+    ts(R("c16", 0, 64), R("ones", 0, 64), -3000.0, None, OP.mult)
+    iota(R("ci", 0, 4), [[-5, 4]], 32, 1)
+    asel(M("BD"), R("ones", 0, 128), [[-16, 8], [0, 16]], OP.is_ge, 0.0, 0, 1)
+    asel(M("BD"), M("BD"), [[16, 8], [0, 16]], OP.is_ge, 0.0, 15, -1)
+    asel(M("I"), R("ones", 0, 128), [[-1, 128]], OP.is_equal, 0.0, 0, 1)
+    asel(M("S1"), M("BD"), [[-1, 128]], OP.is_equal, 0.0, -1, 1)
+    asel(M("S2"), M("BD"), [[-1, 128]], OP.is_equal, 0.0, 15, 1)
+    iota(R("e1", 0, 2048), [[-1, 16], [-16, 8], [0, 16]], 0, 1, [s_x])
+    ts(R("sel", 0, 2048), R("e1", 0, 2048), 0.0, None, OP.is_equal)
+    iota(R("wf", 0, 512), [[2, 512]], me - int(SH), 0, [s_x])
+    cp(R("w16", 0, 512), R("wf", 0, 512))
+    ts(R("w16", 512, 1024), R("wf", 0, 512), 1.0, None, OP.add)
+    iota(R("om", 0, 384), [[-5, 3], [0, 8], [1, 16]], 32, 0, [s_x])
+    iota(R("dw", 0, 16), [[16, 16]], W + 8 - int(SH), 0, [s_x])
+    ts(R("ci", 0, 4), R("ci", 0, 4), 15, None, OP.bitwise_and)
+    cp(R("cc", 0, 4), R("ci", 0, 4))
+    ts(R("cc", 4, 7), R("cc", 0, 3), -BIG, SH + 1, OP.mult, OP.add)
+    ts(col(7), col(0), 0.25, None, OP.mult)
+    ts(col(8), col(0), 4.0, None, OP.is_equal)
+    ts(col(9), col(0), 4.0, 4.0, OP.is_lt, OP.mult)
+    tt(col(9), col(9), col(8), OP.subtract)
+    ts(col(10), col(0), -1024.0, -512.5, OP.mult, OP.add)
+    ts(col(14), col(8), 5120.0, None, OP.mult)
+    tt(col(10), col(10), col(14), OP.add)
+    ts(col(11), col(0), 0.0, None, OP.is_equal)
+    ts(col(12), col(0), 8.0, None, OP.is_equal)
+    ts(col(13), col(0), 0.0, BIG, OP.is_equal, OP.mult)
+    bd8 = g8("BD")
+    for buf, n, wgt in (("zb", 2, col(13)), ("zf", 0, col(9)), ("zf", 1, col(11)), ("zf", 2, col(12))):
+        ts(R(buf, 144 * n + 15, 144 * n + 143, 16), bd8, wgt, None, OP.mult)
+    for nm, of, f in (("NI", "I", -1.0), ("IB", "I", BIG), ("NIB", "I", -BIG), ("I4", "I", 4096.0), ("BDH", "BD", 0.5),
+                      ("NBDH", "BD", -0.5), ("BDB", "BD", BIG), ("NBDB", "BD", -BIG), ("NBD", "BD", -1.0)):
+        ts(M(nm), M(of), f, None, OP.mult)
+    cp(R("b16", 0, 8), bd8)
+    cp(R("b16", 8, 16), bd8)
+    tt(M("S1"), M("S1"), M("S2"), OP.add)
+    tt(M("ISH"), M("S1"), M("I"), OP.add)
+    cp(IF, M("I"))
+    cp(SHF, M("S1"))
+    cp(R("l32", 256, 384), M("BD"))
+    asel(LB, R("l32", 256, 384), [[0, 8], [-1, 16]], OP.is_ge, 0.0, 7, 0, [s_x])
+    asel(LZ, R("l32", 256, 384), [[0, 8], [1, 16]], OP.is_ge, 0.0, -8, 0, [s_x])
+    ts(R("om", 0, 384), R("om", 0, 384), 15, None, OP.bitwise_and)
+    for t in range(RO):
+        ts(M("TR%d" % t), R("om", 128 * t, 128 * t + 128), col(t), BIG, OP.is_gt, OP.mult)
+    tr3 = R("mb", M("TR0")[1], M("TR2")[2])
+    asel(tr3, tr3, [[0, 3], [-16, 8], [0, 16]], OP.is_ge, 0.0, 0, 1)
+    asel(tr3, tr3, [[0, 3], [16, 8], [0, 16]], OP.is_ge, 0.0, 15, -1)
+    asel(tr3, tr3, [[0, 3], [-1, 128]], OP.not_equal, -BIG, 0, 1)
+    ts(R("dw", 0, 16), R("dw", 0, 16), col(0), None, OP.add)
+
+    ts(R("tab", me, me + V), R("sti", 0, V), -SH, None, OP.add, after=[s_b])
+    ms(R("tab", W, TW), SH)
+    ms(R("xt", W, W + 16), 0.0)
+    for (lo, hi, nm, sn, lat) in ((0, D2, "sa", s_a, 4500), (D2, DC, "sb", s_b, 7000), (DC, V, "sh", s_h, 9000)):
+        for n, s in enumerate(others):
+            piece = R("lan", V * s + lo, V * s + hi)
+            arrive(piece, "%s%d" % (nm, s), NE, [sn], lat)
+            if nm == "sh":
+                mm([(R("p%d" % (4 + n), 0, HC), IF, piece)])
+                act(R("tab", piece[1], piece[2]), R("p%d" % (4 + n), 0, HC), AF.Identity)
+            else:
+                cp(R("tab", piece[1], piece[2]), piece)
+    for s in others:
+        arrive(R("xt", V * s, V * s + V), "sx%d" % s, NE, [s_x], 18000)
+
+    TAB, XT = R("tab", 0, W + 8), R("xt", 0, W + 16)
+    ends = [sum(PCH[:i + 1]) for i in range(len(PCH))]
+    flip = [0, 0]
+    for t in range(RO):
+        par = t % 2
+        base[0] = len(ops)
+        own = lambda a, b: R("tab", me + par + 2 * a, me + 2 * b, 2)
+        o1 = ts(R("so", 0, 64), own(0, 64), SH, None, OP.add)
+        o2 = cp(R("s16", 0, 64), own(0, 64), [o1])
+        cp(R("s16", 64, 512), own(64, 512), [o2])
+        ts(R("so", 64, 512), R("s16", 64, 512), SH, None, OP.add)
+        ts(R("non", 0, 512), R("s16", 0, 512), SH, None, OP.is_equal)
+        ms(R("cb", C0 + 4, C0 + 260), SH)
+        v0 = 0
+        for nv in CH:
+            v1 = v0 + nv
+            st = nv // 32
+            dup = 16 // st
+            pc = [i for i in range(len(PCH)) if ends[i] >= v1][0]
+            n = PCH[pc]
+            u0, u1 = ends[pc] - n, ends[pc]
+            U = lambda b: R(b, u0, u1)
+            act(R("gg", 16 * v0, 16 * v1), ("ind", TAB, R("so", v0, v1)), AF.Identity)
+            if v0 == u0:
+                flip[1] += 1
+                hb = "p%d" % (4 + flip[1] % 2)
+                mm([(R(hb, 0, 128, 1, n), U("non"), M("I")), (R(hb, 128, 256, 1, n), U("non"), M("ISH"))], True, False)
+            mm([(R("p2", d, 512, dup), IF, R("w16", 512 * par + v0, 512 * par + v1)) for d in range(dup)])
+            for kp in range(st):
+                cbk = "p%d" % (flip[0] % 2)
+                flip[0] += 1
+                mm([(R(cbk, d, 512, dup), SEL((st * d + kp + 1) % 16), R("s16", v0, v1)) for d in range(dup)])
+                gs = R("gg", 16 * v0 + kp, 16 * v1, st)
+                for eb, tgt, o in (("e1", "p2", 0), ("e2", cbk, 128)):
+                    tt(R(eb, gs[1], gs[2], st), gs, R(tgt, 0, 512), OP.is_equal)
+                    if v1 == u1:
+                        mm([(R(hb, o + k, o + 128, 16, n), R(eb, 16 * u0 + k, 16 * u1, 16), bd8) for k in range(kp, 16, st)],
+                           False, kp == st - 1 and o > 0)
+            v0 = v1
+            if v1 != u1:
+                continue
+            boost[0] = BOOST
+            t1, t2, t3 = R("p6", 0, n), R("p6", n, 2 * n), R("p6", 2 * n, 3 * n)
+            tr = M("TR%d" % t)
+            s1, s2 = R("sg", 256 * pc, 256 * pc + 128, 1, n), R("sg", 256 * pc + 128, 256 * pc + 256, 1, n)
+            a1, ok = R("ao", 2 * u0, 2 * u0 + n), R("ao", 2 * u0 + n, 2 * u1)
+            act(R("sg", 256 * pc, 256 * pc + 256, 1, n), R(hb, 0, 256, 1, n), AF.Sign)
+            idn = R("mb", M("I")[1], M("I")[1] + n, 1, n)
+            b1, b2 = R(hb, 256, 256 + n), R(hb, 256 + n, 256 + 2 * n)
+            mm([(b2, M("NI"), R("ones", 0, n)), (b1, s1, idn), (b2, s1, idn), (b2, s2, idn)])
+            act(R("ao", 2 * u0, 2 * u1), R(hb, 256, 256 + 2 * n), AF.Relu)
+            mm([(t1, IF, U("s16")), (t2, SHF, U("s16")), (t3, IF, R("w16", 512 * par + u0, 512 * par + u1)),
+                (t2, M("NIB"), R("ones", 0, n))], True, False)
+            mm([(t2, M("IB"), a1), (t3, M("NIB"), a1), (t1, tr, ok), (t2, tr, ok), (t3, tr, ok)], False, True)
+            rr = lambda a, b: R("rr", 3 * u0 + a * n, 3 * u0 + b * n)
+            act(rr(0, 3), R("p6", 0, 3 * n), AF.Relu, col(4 + t))
+            bz = R("p7", 0, n)
+            mm([(bz, LB, rr(0, 1)), (bz, LZ, rr(1, 2)), (bz, LZ, rr(2, 3))])
+            act(U("ab"), bz, AF.Abs, col(10))
+            act(U("bzs"), bz, AF.Identity, -SH - 1)
+            ts(U("ind"), U("ab"), 512.0, None, OP.is_lt)
+            scan(U("val"), U("ind"), U("ind"), col(7) if u0 == 0 else R("val", u0 - 1, u0), OP.add, OP.max)
+            scan(U("prod"), U("val"), U("ind"), 0.0, OP.max, OP.mult)
+            ob = R("p3", 0, n // 16)
+            mm([(ob, Z("zf", 0, a), R("prod", u0 + a, u1, 16)) for a in range(16)])
+            ts(R("co", u0 // 16, u1 // 16), ob, float(C0), None, OP.add)
+            scat(R("cb", 0, 2576), R("co", u0 // 16, u1 // 16), U("bzs"))
+            boost[0] = 0.0
+        for o in range(N):
+            cp(R("c16", 64 + 64 * o, 128 + 64 * o), R("cb", C0 + 4 + o, C0 + 260, 4))
+        mm([(R("p7", 0, 16), Z("zf", 1, a), R("c16", 64 + a, 320, 16)) for a in range(16)])
+        mm([(R("p3", 0, 16), Z("zf", 2, a), R("c16", 64 + a, 320, 16)) for a in range(16)])
+        ts(R("obz", 0, 16), R("p7", 0, 16), SH, None, OP.add)
+        for lo, hi in ((0, 64), (64, 256)):
+            ts(R("eo", lo, hi), ("ind", TAB, R("obz", lo // 16, hi // 16)), SH, None, OP.add)
+        ts(R("obz", 16, 32), R("p3", 0, 16), SH, None, OP.add)
+        for o in (256, 0):
+            cp(R("xbz", o, o + 128), ("ind", XT, R("obz", o // 16, o // 16 + 8)))
+        boost[0] = DB
+        mm([(R("p3", 0, 256), SEL(0), R("c16", 64, 320))])
+        act(R("bbs", 0, 256), R("p3", 0, 256), AF.Identity)
+        act(R("inv", 0, 256), R("p3", 0, 256), AF.Relu, 1.0 - SH)
+        for q in range(4):
+            mm([(R("p1", 0, 304), Z("zf", 1, a), R("c16", 15 - a, 319 - a)) for a in range(4 * q, 4 * q + 4)], q == 0, q == 3)
+        for q in range(4):
+            tt(R("eq", 256 * q, 256 * q + 256), R("bbs", 0, 256), R("p1", 48 - 16 * q, 304 - 16 * q), OP.is_equal)
+        mm([(R("p3", 0, 256), M("I"), R("inv", 0, 256))] + [(R("p3", 0, 256), M("BD"), R("eq", 256 * q, 256 * q + 256)) for q in range(4)])
+        act(R("cnt", 0, 256), R("p3", 0, 256), AF.Identity)
+        mm([(R("p1", 0, 16), Z("zf", 1, a), R("c16", 64 + a, 320, 16)) for a in range(16)], True, False)
+        mm([(R("p1", 0, 16), Z("zb", 2, a), R("cnt", a, 256, 16)) for a in range(16)], False, True)
+        boost[0] = BOOST
+        tt(R("tg", 0, 16), R("dw", 0, 16), R("p1", 0, 16), OP.min)
+        mo = lambda s: 64 * t + 16 * s
+        md = lambda s: 1024 * t + 256 * s
+        ts(R("mo", mo(rank), mo(rank) + 16), R("tg", 0, 16), SH, None, OP.add)
+        s_o = send([(R("mo", mo(rank), mo(rank) + 16), peers)], "mo%d%d" % (t, rank), off_eng)
+        boost[0] = 0.0
+        for s in others:
+            arrive(R("mo", mo(s), mo(s) + 16), "mo%d%d" % (t, s), NE, [s_o], 3000)
+        last, sent = [], []
+        for h in range(2):
+            s0 = 128 * h
+            H = lambda b, o=0: R(b, o + s0, o + s0 + 128)
+            K = lambda b, k: R(b, 16 * s0 + k, 16 * s0 + 2048, 16)
+            hb = "p%d" % (4 + h)
+            r2, r1 = R(hb, 0, 128), R(hb, 128, 256)
+            for q in range(2):
+                c0 = s0 + 64 * q
+                act(R("xe", 16 * c0, 16 * c0 + 1024), ("ind", XT, R("eo", c0, c0 + 64)), AF.Identity)
+                if q == 0:
+                    if h == 1:
+                        for o in (384, 128):
+                            act(R("xbz", o, o + 128), ("ind", XT, R("obz", o // 16, o // 16 + 8)), AF.Identity)
+                    act(H("sbf"), ("ind", TAB, R("obz", 8 * h, 8 * h + 8)), AF.Identity)
+                    act(H("nj"), H("sbf"), AF.Relu, 1.0 - SH)
+                    mm([(R("p7", 0, 128), M("I"), H("xbz", 256)), (R("p7", 0, 128), M("NI"), H("xbz"))])
+                    act(H("dzb"), R("p7", 0, 128), AF.Abs)
+                mm([(R("p0", d, 512, 8), M("I"), R("xbz", 256 + c0, 320 + c0)) for d in range(8)])
+                mm([(R("p2", d, 512, 8), M("I"), R("xbz", c0, c0 + 64)) for d in range(8)])
+                if q == 1:
+                    mm([(r2, H("nj"), M("IB")), (r1, H("nj"), M("IB")), (r2, H("xbz", 256), M("NBDH")), (r2, H("xbz"), M("BDH")),
+                        (r1, H("xbz", 256), M("NBDH")), (r1, H("dzb"), M("NBDH"))], True, False)
+                    for kp in range(2):
+                        mm([(R(hb, 128 + k, 256, 16), K("xe", k), g8("NBDH")) for k in range(kp, 16, 2)], False, False)
+                for kp in range(2):
+                    xs = R("xe", 16 * c0 + kp, 16 * c0 + 1024, 2)
+                    for eb, tgt, hi, w8 in (("e1", "p0", 256, R("b16", 0, 16)), ("e2", "p2", 128, g8("NBD"))):
+                        tt(R(eb, xs[1], xs[2], 2), xs, R(tgt, 0, 512), OP.max)
+                        if q == 1:
+                            mm([(R(hb, k, hi, 16), K(eb, k), w8) for k in range(kp, 16, 2)], False, kp == 1 and eb == "e2")
+            boost[0] = BOOST
+            pu, px = R("p6", 0, 128), R("p6", 128, 256)
+            mm([(pu, M("I4"), R("mhalf", 0, 128)), (px, SEL(8), H("c16", 64)), (px, M("IB"), R("ones", 0, 128)), (px, M("TR0"), H("nj"))], True, False)
+            f0 = 2 * s0
+            ev, rf = R("er", f0, f0 + 128), R("er", f0 + 128, f0 + 256)
+            act(R("fl", f0, f0 + 256), R(hb, 0, 256), AF.Sign)
+            mm([(R(hb, 256, 384), R("fl", f0, f0 + 128), M("NI")), (R(hb, 384, 512), R("fl", f0 + 128, f0 + 256), M("NI"))])
+            act(R("er", f0, f0 + 256), R(hb, 256, 512), AF.Relu)
+            mm([(pu, M("NBDB"), rf), (px, M("BDB"), rf), (pu, M("I4"), ev), (px, M("TR0"), ev)], False, True)
+            tt(H("uu"), H("sbf"), pu, OP.max)
+            last.append(tt(H("md", md(rank)), H("uu"), px, OP.min))
+            sem = "md%d%d%d" % (t, h, rank)
+            if t < RO - 1:
+                sent.append(send([(H("md", md(rank)), peers)], sem, off_eng))
+            else:
+                sent.append(send([(R("md", md(rank) + 64 * o, md(rank) + 64 * o + 64), [T.cores[o]]) for o in (2 * h, 2 * h + 1) if o != rank],
+                                 sem, off_eng))
+            boost[0] = 0.0
+        for h in range(2):
+            if t == RO - 1 and h != rank // 2:
+                continue
+            lo, n = (128 * h, 128) if t < RO - 1 else (64 * rank, 64)
+            for s in range(N - 1, -1, -1):
+                dat = R("md", md(s) + lo, md(s) + lo + n)
+                if s != rank:
+                    arrive(dat, "md%d%d%d" % (t, h, s), NE if t < RO - 1 or s // 2 == h else NE // 2, [sent[h]], 3500)
+                scat(R("tab", 0, TW), R("mo", mo(s) + lo // 16, mo(s) + (lo + n) // 16), dat, [last[1]])
+    act(R("yb", 0, 512), R("tab", me, me + 512), AF.Identity, SH)
+    ts(R("yb", 512, V), R("tab", me + 512, me + V), SH, None, OP.add)
+    add("a", lambda: g.scalar.dma_start(T.y[:, 0:512], T.yb[:, 0:512]), 50, [R("yb", 0, 512)], [], sem="st0", val=16, lat=2500)
+    add("s", lambda: g.sync.dma_start(T.y[:, 512:V], T.yb[:, 512:V]), 50, [R("yb", 512, V)], [], sem="st1", val=16, lat=2500)
+    return ops, Q, nloc[0]
+
+
+def order(ops, kids, pr, noise):
+    n = len(ops)
+    left = [len(o["deps"]) for o in ops]
+    key = [pr[i] + ops[i]["boost"] + noise.get(ops[i]["tag"], 0.0) for i in range(n)]
+    rdy = [0.0] * n
+    pool = {e: [] for e in "vapgsx"}
+    free = {e: 0.0 for e in "vapgsx"}
+    for i in range(n):
+        if left[i] == 0:
+            pool[ops[i]["eng"]].append(i)
+    seq = []
+    while len(seq) < n:
+        best = None
+        for e in pool:
+            if pool[e]:
+                t0 = max(free[e], min(rdy[i] for i in pool[e]))
+                if best is None or t0 < best[0]:
+                    best = (t0, e)
+        t0, e = best
+        i = max([i for i in pool[e] if rdy[i] <= t0 + LOOK], key=lambda i: key[i])
+        pool[e].remove(i)
+        t0 = max(t0, rdy[i])
+        if e != "x":
+            free[e] = t0 + ops[i]["cost"]
+        done = t0 + ops[i]["cost"] + max(ops[i]["lat"], 0.0)
+        seq.append(i)
+        for k in kids[i]:
+            rdy[k] = max(rdy[k], done + (HOP if ops[k]["deps"][i] else 0.0))
+            left[k] -= 1
+            if left[k] == 0:
+                pool[ops[k]["eng"]].append(k)
+    return seq
+
+
+def span(ops, seq, pe, ga, hop):
+    done = [0.0] * len(ops)
+    free = {e: 0.0 for e in "vapgsx"}
+    for i in seq:
+        o = ops[i]
+        t0 = max([free[o["eng"]]] + [done[j] + (hop if h else 0.0) for j, h in o["deps"].items()])
+        c = o["cost"] * (pe if o["pe"] else 1.0) + CYC * (ga - GA) * o["ga"]
+        if o["eng"] != "x":
+            free[o["eng"]] = t0 + c
+        done[i] = t0 + c + max(o["lat"], 0.0)
+    return max(done), done
+
+
+FOUND = {}
+
+
+def plan(ops):
+    n = len(ops)
+    kids = [[] for _ in range(n)]
+    for i, o in enumerate(ops):
+        for j in o["deps"]:
+            kids[j].append(i)
+    pr = [0.0] * n
+    for i in range(n - 1, -1, -1):
+        pr[i] = ops[i]["cost"] + max(ops[i]["lat"], 0.0) + max([pr[k] + HOP for k in kids[i]] + [0.0])
+    score = lambda q: sum(span(ops, q, *f)[0] for f in FIGS)
+    if "noise" not in FOUND:
+        rng = np.random.default_rng(1)
+        tags = sorted(set(o["tag"] for o in ops))
+        noise = {}
+        best = score(order(ops, kids, pr, noise))
+        for _ in range(TRIES):
+            cand = dict(noise)
+            for k in rng.choice(len(tags), 6):
+                cand[tags[int(k)]] = float(rng.normal()) * float(rng.choice([1000.0, 5000.0, 30000.0]))
+            val = score(order(ops, kids, pr, cand))
+            if val <= best:
+                best, noise = val, cand
+        FOUND["noise"] = noise
+    return order(ops, kids, pr, FOUND["noise"])
+
+
+def emit(g, T, ops, Q, nloc):
+    seq = plan(ops)
+    need = set(j for o in ops for j, hard in o["deps"].items() if hard)
+    count = {e: 0 for e in "vapg"}
+    tok, seen = {}, {}
+    for i in seq:
+        o = ops[i]
+        e = o["eng"]
+        if e == "x":
+            tok[i] = (o["sem"], o["val"])
+            continue
+        want = {}
+        for j, hard in o["deps"].items():
+            if hard and tok[j] is not None:
+                want[tok[j][0]] = max(want.get(tok[j][0], 0), tok[j][1])
+        for s, v in want.items():
+            if seen.get((e, s), 0) < v:
+                Q[e].wait_ge(T.sem[s], v)
+                seen[(e, s)] = v
+        ins = o["fn"]()
+        if o["sem"] is not None:
+            ins.then_inc(T.sem[o["sem"]], 16)
+            tok[i] = (o["sem"], o["val"])
+        elif o["lat"] < 0:
+            tok[i] = None
+        elif i in need:
+            count[e] += 1
+            ins.then_inc(T.sem["q" + e], 1)
+            tok[i] = ("q" + e, count[e])
+    for e in count:
+        g.wait_ge(T.sem["q" + e], count[e])
+    g.wait_ge(T.sem.loc, nloc)
+    g.wait_ge(T.sem.st0, 16)
+    g.wait_ge(T.sem.st1, 16)
+
+
+def rank_program(g, core, T, topo):
+    if T.rank_of(core) is not None:
+        ops, Q, nloc = build(g, core, T, topo)
+        emit(g, T, ops, Q, nloc)
+        return
+    for rank, c in enumerate(T.cores):
+        peers = [p for p in T.cores if p != c]
+        if helper_of(c, peers, topo) == core:
+            own = common_engines(c, peers, topo)
+            eng = common_engines(core, peers, topo)
+            g.wait_ge(T.sem.hin, len([e for e in topo.engines(c, core) if e not in own]))
+            g.remote_dma_fused([transfer(topo, peers, T.lan[:, V * rank + V - HC:V * rank + V], T.sem["sh%d" % rank], eng)], local_sem=T.sem.loc)
+            g.wait_ge(T.sem.loc, len(eng))

@@ -1,45 +1,44 @@
-import numpy as np
 from concourse.bass import DstId, RemoteDMATransfer
 from concourse.mybir import AluOpType as OP, ActivationFunctionType as AF
 
 N, V, W, RO = 4, 1024, 4096, 3
 SH = 2048.0
 BIG = 8192.0
-TW = W + 8 + 256
+TW = W + 8 + 512
 C0 = 520
-HC = 384
 CH = [32, 32] + [64] * 7
 PCH = [128, 128, 128, 128]
-BOOST, DB, LOOK, TRIES = 30000.0, 5000.0, 100.0, 1200
-CYC, PEC, GA, SC, HOP = 1.04, 0.52, 1.56, 3.8, 120.0
-FIGS = ((1.0, 1.56, 120.0), (0.85, 1.15, 200.0), (1.15, 2.0, 70.0))
-MATS = ["I", "NI", "IB", "NIB", "ISH", "BDH", "NBDH", "BDB", "NBDB", "I4", "TR0", "TR1", "TR2", "BD", "S1", "S2", "NBD"]
+VCH = [384, 128]
+SUB = [64, 64, 64, 64]
+JC = [[128, 128], [128, 128], [128, 64, 64]]
+ABS = [[(1, 1)], [(1, 1)], []]
+CYC, PEC, GA, SC, HOP, LOOK = 0.83, 0.42, 1.56, 3.8, 100.0, 100.0
+RL = 60000.0
+DUE = {"test": 1700, "sel": [1300, 11400, 12100, 17500], "pack": [30300, 31700], "mo": 30300, "max": 25400, "abs": -2900,
+       "md": [29400, 31000, 44100], "tab": [42300, 36300], "const": -2300, "load": -19500}
+MATS = ["I", "NI", "IB", "NIB", "ISH", "BDH", "NBDH", "BDB", "NBDB", "I4", "TR0", "TR1", "TR2", "BD", "S1", "S2", "NBD", "I3"]
 F, B, H16, U16, I32 = "float32", "bfloat16", "float16", "uint16", "int32"
 SCRATCH = {n: ("sbuf", [128, w], d) for n, w, d in [
-    ("sti", V, I32), ("lan", W, H16), ("tab", TW, F), ("xt", W + 16, B), ("gg", 8192, F), ("e1", 8192, B), ("e2", 8192, B),
+    ("sti", V, I32), ("out", V, H16), ("lan", V, H16), ("xs", V, B), ("xl", V, B), ("io1", 512, B), ("io2", 512, B), ("un", 512, H16),
+    ("rep", 512, H16), ("pq", 896, H16), ("cm", 16, F), ("ai", 64, I32), ("ao2", 64, U16), ("stg", V, F), ("ls", V, F), ("mf32", 1024, F),
+    ("lm", 256, H16), ("lt", 64, H16), ("tab", TW, F), ("xt", W + 16, B), ("gg", 8192, F), ("e1", 8192, B), ("e2", 8192, B),
     ("xe", 4096, B), ("mb", 128 * len(MATS), B), ("sel", 2048, H16), ("mf", 256, H16), ("l32", 384, F), ("zb", 432, B),
-    ("zf", 432, H16), ("ones", 256, B), ("mhalf", 128, B), ("cc", 16, F), ("ci", 4, I32), ("om", 384, I32), ("wf", 512, F),
+    ("zf", 432, H16), ("ones", 256, B), ("mhalf", 128, B), ("cc", 24, F), ("ci", 8, I32), ("om", 384, I32), ("wf", 512, F),
     ("w16", 1024, H16), ("dw", 16, F), ("s16", 512, H16), ("so", 512, U16), ("non", 512, B), ("sg", 1536, B), ("ao", 1024, B),
-    ("b16", 16, B), ("rr", 1536, F), ("bzs", 512, F), ("ab", 512, F), ("ind", 512, H16), ("val", 512, F), ("prod", 512, H16),
-    ("co", 32, U16), ("cb", 2576, F), ("c16", 320, H16), ("obz", 32, U16), ("eo", 256, U16), ("xbz", 512, B), ("sbf", 256, F),
-    ("nj", 256, B), ("dzb", 256, B), ("fl", 512, B), ("er", 512, B), ("uu", 256, F), ("bbs", 256, F), ("inv", 256, B),
-    ("eq", 1024, B), ("cnt", 256, B), ("tg", 16, F), ("md", RO * 1024, H16), ("mo", RO * 64, U16), ("yb", V, F)]}
+    ("b16", 32, B), ("rr", 1536, F), ("ab", 512, F), ("ind", 512, H16), ("val", 512, H16), ("prod", 512, H16),
+    ("co", 32, U16), ("cb", 2576, F), ("c16", 320, H16), ("obz", 32, U16), ("eo", 256, U16), ("xbz", 512, B), ("sbf", 256, H16),
+    ("nj", 256, B), ("dzb", 256, B), ("fl", 768, B), ("er", 512, B), ("uu", 256, H16), ("shf", 304, H16), ("bl", 16, H16),
+    ("eq", 1024, B), ("cnt", 256, B), ("tg", 16, H16), ("md", 256, H16), ("mo", 64, U16), ("yb", TW, F)]}
 for _i in range(8):
     SCRATCH["p%d" % _i] = ("psum", [128, 512], F)
-SEMAPHORES = ["qv", "qa", "qp", "qg", "ld0", "ld1", "ldx", "st0", "st1", "loc", "hin"]
+SEMAPHORES = ["qv", "qa", "qp", "qg", "ldx", "xt", "yb", "sf", "st0", "st1", "loc"]
 for _s in range(N):
-    SEMAPHORES += ["sa%d" % _s, "sb%d" % _s, "sh%d" % _s, "sx%d" % _s]
-    for _t in range(RO):
-        SEMAPHORES += ["mo%d%d" % (_t, _s), "md%d0%d" % (_t, _s), "md%d1%d" % (_t, _s)]
+    SEMAPHORES += [_n + str(_s) for _n in ("ld", "sa", "sx", "sy", "sg", "lm", "lt")]
 
 
-def helper_of(c, peers, topo):
-    return [h for h in topo.cores_of(c) if topo.die(h) != topo.die(c) and all(topo.may_write(h, p) for p in peers)][0]
-
-
-def transfer(topo, dst_cores, ap, sem, engines):
+def transfer(topo, dst_cores, src, dst, sem, engines):
     ids = [DstId(rid=topo.addr(d)[0], pnc=topo.addr(d)[1]) for d in dst_cores]
-    return RemoteDMATransfer(dst_ids=ids, dma_engine_mask=sum(1 << e for e in engines), remote_sem=sem, srcs=[ap], dsts=[ap] * len(ids))
+    return RemoteDMATransfer(dst_ids=ids, dma_engine_mask=sum(1 << e for e in engines), remote_sem=sem, srcs=[src], dsts=[dst] * len(ids))
 
 
 def common_engines(src, dsts, topo):
@@ -58,13 +57,17 @@ def bits(r):
     return (((1 << (width(r) * r[3])) - 1) // ((1 << r[3]) - 1)) << r[1]
 
 
+def parts(sizes):
+    ends = [sum(sizes[:i + 1]) for i in range(len(sizes))]
+    return [(e - n, e) for e, n in zip(ends, sizes)]
+
+
 def build(g, core, T, topo):
     rank = T.rank_of(core)
     peers = [c for c in T.cores if c != core]
-    others = [s for s in range(N) if s != rank]
     off_eng = common_engines(core, peers, topo)
     NE = len(off_eng)
-    ops, acc, nloc, boost, base = [], {}, [0], [0.0], [-1000]
+    ops, acc, nloc, base, ndma, soon = [], {}, [0], [-1000], {}, [None]
     Q = {"v": g.vector, "a": g.scalar, "p": g.tensor, "g": g, "s": g.sync}
 
     def ap(r):
@@ -93,8 +96,8 @@ def build(g, core, T, topo):
             acc[r[0]] = keep
         for j in after:
             deps[j] = deps.get(j, False)
-        ops.append({"eng": eng, "fn": fn, "cost": cost, "deps": deps, "sem": sem, "val": val, "lat": lat, "boost": boost[0],
-                    "tag": i - base[0], "ga": ga, "pe": eng == "p"})
+        ops.append({"eng": eng, "fn": fn, "cost": cost, "deps": deps, "sem": sem, "val": val, "lat": lat,
+                    "tag": i - base[0], "ga": ga, "pe": eng == "p", "due": RL * RO if soon[0] is None else soon[0]})
         return i
 
     def sc(x):
@@ -108,7 +111,7 @@ def build(g, core, T, topo):
     def two(*rs):
         return all(SCRATCH[r[0]][2] in (B, H16, U16) for r in rs)
 
-    def ts(out, in0, s1, s2, o0, o1=None, after=()):
+    def ts(out, in0, s1, s2, o0, o1=None):
         a, rd, f = src(in0)
         if f == 1.0 and two(out, in0):
             f = 0.5
@@ -117,32 +120,33 @@ def build(g, core, T, topo):
             fn = lambda: g.vector.tensor_scalar(ap(out), a, sc(s1), None, o0)
         else:
             fn = lambda: g.vector.tensor_scalar(ap(out), a, sc(s1), sc(s2), o0, o1)
-        return add("v", fn, 60 + CYC * max(64, f * width(out)), rd, [out], after)
+        return add("v", fn, 60 + CYC * max(64, f * width(out)), rd, [out], ga=width(out) if f == GA else 0)
 
-    def tt(out, a, b, o, after=()):
+    def tt(out, a, b, o):
         f = 1 if SCRATCH[b[0]][0] == "psum" else 2
-        return add("v", lambda: g.vector.tensor_tensor(ap(out), ap(a), ap(b), o), 60 + CYC * max(64, f * width(out)), [a, b], [out], after)
+        return add("v", lambda: g.vector.tensor_tensor(ap(out), ap(a), ap(b), o), 60 + CYC * max(64, f * width(out)), [a, b], [out])
 
-    def cp(out, in_, after=()):
+    def cp(out, in_):
         a, rd, f = src(in_)
         if f == 1.0 and two(out, in_):
             f = 0.5
-        return add("v", lambda: g.vector.tensor_copy(ap(out), a), 60 + CYC * max(64, f * width(out)), rd, [out], after)
+        return add("v", lambda: g.vector.tensor_copy(ap(out), a), 60 + CYC * max(64, f * width(out)), rd, [out], ga=width(out) if f == GA else 0)
 
-    def scat(win, off, a, after=()):
-        return add("v", lambda: g.vector.tensor_copy(ap(win).indirect(ap(off)), ap(a)), 60 + CYC * SC * width(a), [off, a], [win], after)
+    def scat(win, off, a):
+        return add("v", lambda: g.vector.tensor_copy(ap(win).indirect(ap(off)), ap(a)), 60 + CYC * SC * width(a), [off, a], [win])
 
     def ms(out, c):
         return add("v", lambda: g.vector.memset(ap(out), c), 60 + CYC * max(64, width(out)), [], [out])
 
     def scan(out, d0, d1, init, o0, o1):
         rd = [d0, d1] + ([init] if isinstance(init, tuple) else [])
-        return add("v", lambda: g.vector.tensor_tensor_scan(ap(out), ap(d0), ap(d1), sc(init), o0, o1), 60 + CYC * max(64, width(out)), rd, [out])
+        f = 0.5 if two(out, d0, d1) else 1.0
+        return add("v", lambda: g.vector.tensor_tensor_scan(ap(out), ap(d0), ap(d1), sc(init), o0, o1), 60 + CYC * max(64, f * width(out)), rd, [out])
 
-    def act(out, in_, func, bias=0.0, after=()):
+    def act(out, in_, func, bias=0.0, scale=1.0):
         a, rd, f = src(in_)
         rd = rd + ([bias] if isinstance(bias, tuple) else [])
-        return add("a", lambda: g.scalar.activation(ap(out), a, func, bias=sc(bias)), 80 + CYC * max(64, f * width(out)), rd, [out], after,
+        return add("a", lambda: g.scalar.activation(ap(out), a, func, bias=sc(bias), scale=scale), 80 + CYC * max(64, f * width(out)), rd, [out],
                    ga=width(out) if f == GA else 0)
 
     def mm(terms, start=True, stop=True):
@@ -163,19 +167,33 @@ def build(g, core, T, topo):
     def asel(out, a, pat, cmp, fill, start, cm, after=()):
         return add("g", lambda: g.affine_select(ap(out), ap(a), pat, cmp, fill, start, cm), 200 + 2 * CYC * width(out), [a], [out], after)
 
-    def send(parts, sem, engines, after=()):
-        k = len(engines) // len(parts)
-        nloc[0] += k * len(parts)
-        fn = lambda: g.remote_dma_fused([transfer(topo, d, ap(r), T.sem[sem], engines[k * n:k * n + k]) for n, (r, d) in enumerate(parts)],
-                                        local_sem=T.sem.loc)
-        return add("g", fn, 700, [r for r, d in parts], [], after, lat=-1.0)
+    def send(pieces, sem, engines, after=()):
+        k = 1 << (len(engines) // len(pieces)).bit_length() - 1
+        nloc[0] += k * len(pieces)
+        fn = lambda: g.remote_dma_fused([transfer(topo, d, ap(r), ap(to), T.sem[sem], engines[k * n:k * n + k])
+                                         for n, (r, to, d) in enumerate(pieces)], local_sem=T.sem.loc)
+        return add("g", fn, 700, [r for r, to, d in pieces], [], after, lat=-1.0), k
+
+    def dma(q, out, in_, rd, wr, sem, lat, after=()):
+        ndma[sem] = ndma.get(sem, 0) + 16
+        i = add(q, lambda: Q[q].dma_start(out, in_), 50, rd, wr, sem=sem, val=ndma[sem], lat=lat)
+        for j in after:
+            ops[i]["deps"][j] = True
+        return i
 
     def arrive(r, sem, val, after, lat):
         return add("x", None, 0, [], [r], after, sem=sem, val=val, lat=lat)
 
-    def M(name):
+    def landed(r, sem):
+        return add("x", None, 0, [], [r], [i for i, o in enumerate(ops) if o["sem"] == sem], sem=sem, val=ndma[sem])
+
+    def due(i, at):
+        ops[i]["due"] = at
+        return i
+
+    def M(name, n=128):
         k = MATS.index(name)
-        return R("mb", 128 * k, 128 * k + 128)
+        return R("mb", 128 * k, 128 * k + n, 1, n)
 
     def g8(name):
         return R("mb", M(name)[1], M(name)[2], 16)
@@ -186,74 +204,98 @@ def build(g, core, T, topo):
     def SEL(k):
         return R("sel", 128 * k, 128 * k + 128)
 
+    def PQ(s, q):
+        return R("pq", 224 * q + 96 - 32 * s, 224 * q + 224 - 32 * s)
+
     def col(k):
         return R("cc", k, k + 1)
 
-    me = V * rank
-    DC = V - HC
-    D2 = DC // 2
     IF, SHF = R("mf", 0, 128), R("mf", 128, 256)
     LB, LZ = R("l32", 0, 128), R("l32", 128, 256)
-    boost[0] = BOOST
-    add("s", lambda: g.sync.dma_start(T.sti[:, DC:V], T.stars[:, DC:V]), 50, [], [R("sti", DC, V)], sem="ld0", val=16, lat=2600)
-    add("a", lambda: g.scalar.dma_start(T.sti[:, 0:DC], T.stars[:, 0:DC]), 50, [], [R("sti", 0, DC)], sem="ld1", val=16, lat=3200)
-    add("s", lambda: g.sync.dma_start(T.xt[:, me:me + V], T.x[:, :]), 50, [], [R("xt", me, me + V)], sem="ldx", val=16, lat=4000)
-    hp = helper_of(core, peers, topo)
-    ts(R("lan", me + DC, me + V), R("sti", DC, V), -SH, None, OP.add)
-    s_h = send([(R("lan", me + DC, me + V), [hp])], "hin", [e for e in topo.engines(core, hp) if e not in off_eng])
-    ts(R("lan", me, me + D2), R("sti", 0, D2), -SH, None, OP.add)
-    s_a = send([(R("lan", me, me + D2), peers)], "sa%d" % rank, off_eng, [s_h])
-    ts(R("lan", me + D2, me + DC), R("sti", D2, DC), -SH, None, OP.add)
-    s_b = send([(R("lan", me + D2, me + DC), peers)], "sb%d" % rank, off_eng, [s_a])
-    s_x = send([(R("xt", me, me + V), peers)], "sx%d" % rank, off_eng, [s_b])
-    boost[0] = 0.0
+    ring = [(rank + 1 + j) % N for j in range(N)]
+    blk = lambda b, d, n=256: R(b, n * d, n * d + n)
+    rows = lambda d: slice(32 * d, 32 * d + 32)
+    soon[0] = DUE["load"]
+    lds = [dma("sa"[n % 2], ap(blk("sti", d)), T.stars[rows(d), :], [], [blk("sti", d)], "ld%d" % d, 2400 + 100 * n) for n, d in enumerate(ring)]
+    s_a = []
+    for d in ring[:-1]:
+        ts(blk("out", d), blk("sti", d), -SH, None, OP.add)
+        s_a.append(send([(blk("out", d), blk("lan", rank), [T.cores[d]])], "sa%d" % rank, off_eng, s_a[-1:])[0])
+    ts(blk("lan", rank), blk("sti", rank), -SH, None, OP.add)
+    soon[0] = DUE["const"]
+    for d in ring[:-1]:
+        dma("s", ap(blk("xs", d)), T.x[rows(d), :], [], [blk("xs", d)], "ldx", 2500, lds)
+    landed(R("xs", 0, V), "ldx")
+    s_x, kx = send([(blk("xs", d), blk("xl", rank), [T.cores[d]]) for d in ring[:-1]], "sx%d" % rank, off_eng, s_a[-1:])
+    for s in ring[::-1]:
+        if s != rank:
+            arrive(blk("xl", s), "sx%d" % s, kx, [s_x], 6000)
+        for q in range(N):
+            if s == rank:
+                dma("s", T.xt[rows(q), V * s:V * s + V], T.x[rows(s), :], [], [], "xt", 2500, lds)
+            else:
+                dma("s", T.xt[rows(q), V * s:V * s + V], ap(blk("xl", s)), [blk("xl", s)], [], "xt", 3000)
+    landed(R("xt", 0, W), "xt")
 
     ms(R("ones", 0, 256), 1.0)
     ms(R("mhalf", 0, 128), -0.5)
     ms(R("zb", 0, 432), 0.0)
     ts(R("zf", 0, 432), R("zb", 0, 432), 0.0, None, OP.mult)
     ts(R("c16", 0, 64), R("ones", 0, 64), -3000.0, None, OP.mult)
-    iota(R("ci", 0, 4), [[-5, 4]], 32, 1)
+    iota(R("ci", 0, 8), [[0, 2], [-5, 4]], 32, 1)
+    iota(R("io1", 0, 512), [[-1, 4], [0, 4], [-4, 32]], 0, 1)
+    ts(R("un", 0, 512), R("io1", 0, 512), 0.0, None, OP.is_equal)
     asel(M("BD"), R("ones", 0, 128), [[-16, 8], [0, 16]], OP.is_ge, 0.0, 0, 1)
     asel(M("BD"), M("BD"), [[16, 8], [0, 16]], OP.is_ge, 0.0, 15, -1)
     asel(M("I"), R("ones", 0, 128), [[-1, 128]], OP.is_equal, 0.0, 0, 1)
-    asel(M("S1"), M("BD"), [[-1, 128]], OP.is_equal, 0.0, -1, 1)
-    asel(M("S2"), M("BD"), [[-1, 128]], OP.is_equal, 0.0, 15, 1)
-    iota(R("e1", 0, 2048), [[-1, 16], [-16, 8], [0, 16]], 0, 1, [s_x])
-    ts(R("sel", 0, 2048), R("e1", 0, 2048), 0.0, None, OP.is_equal)
-    iota(R("wf", 0, 512), [[2, 512]], me - int(SH), 0, [s_x])
-    cp(R("w16", 0, 512), R("wf", 0, 512))
-    ts(R("w16", 512, 1024), R("wf", 0, 512), 1.0, None, OP.add)
-    iota(R("om", 0, 384), [[-5, 3], [0, 8], [1, 16]], 32, 0, [s_x])
-    iota(R("dw", 0, 16), [[16, 16]], W + 8 - int(SH), 0, [s_x])
+    late = s_a[-1:]
+    asel(M("S1"), M("BD"), [[-1, 128]], OP.is_equal, 0.0, -1, 1, late)
+    asel(M("S2"), M("BD"), [[-1, 128]], OP.is_equal, 0.0, 15, 1, late)
+    iota(R("wf", 0, 512), [[2, 512]], -int(SH), 0, late)
+    iota(R("ai", 0, 64), [[1, 2], [32, 32]], 0, 0, late)
+    iota(R("om", 0, 384), [[-5, 3], [0, 8], [1, 16]], 32, 0, late)
+    iota(R("dw", 0, 16), [[32, 16]], W + 8 - int(SH), 0, late)
+    iota(R("cm", 0, 16), [[1, 16]], 0, 0)
+    ts(R("ci", 5, 6), R("ci", 4, 5), rank + 1, None, OP.add)
+    ts(R("ci", 5, 6), R("ci", 5, 6), 3, None, OP.bitwise_and)
+    ts(R("ci", 4, 5), R("ci", 4, 5), 5, None, OP.arith_shift_right)
+    cp(R("cc", 16, 18), R("ci", 4, 6))
     ts(R("ci", 0, 4), R("ci", 0, 4), 15, None, OP.bitwise_and)
     cp(R("cc", 0, 4), R("ci", 0, 4))
-    ts(R("cc", 4, 7), R("cc", 0, 3), -BIG, SH + 1, OP.mult, OP.add)
-    ts(col(7), col(0), 0.25, None, OP.mult)
+    ts(R("cc", 4, 7), R("cc", 0, 3), -BIG, SH + 1 - BIG, OP.mult, OP.add)
+    ts(col(14), col(0), 4.0, None, OP.is_lt)
+    ts(col(7), col(14), col(0), 512.0, OP.mult, OP.mult)
     ts(col(8), col(0), 4.0, None, OP.is_equal)
-    ts(col(9), col(0), 4.0, 4.0, OP.is_lt, OP.mult)
-    tt(col(9), col(9), col(8), OP.subtract)
-    ts(col(10), col(0), -1024.0, -512.5, OP.mult, OP.add)
-    ts(col(14), col(8), 5120.0, None, OP.mult)
-    tt(col(10), col(10), col(14), OP.add)
-    ts(col(11), col(0), 0.0, None, OP.is_equal)
-    ts(col(12), col(0), 8.0, None, OP.is_equal)
-    ts(col(13), col(0), 0.0, BIG, OP.is_equal, OP.mult)
+    ts(col(9), col(14), col(8), None, OP.subtract)
+    ts(col(10), col(17), -1024.0, -512.5, OP.mult, OP.add)
+    ts(col(10), col(10), col(14), None, OP.mult)
+    ts(col(10), col(8), 511.5, col(10), OP.mult, OP.add)
+    ts(col(16), col(16), 1024.0, -1024.0, OP.mult, OP.add)
+    ts(R("w16", 0, 512), R("wf", 0, 512), col(16), None, OP.add)
+    ts(col(18), col(0), 2.0, col(16), OP.mult, OP.add)
+    ts(R("ao2", 0, 64), R("ai", 0, 64), col(18), None, OP.add)
+    ts(R("cm", 0, 16), R("cm", 0, 16), col(0), None, OP.is_equal)
+    ts(col(21), col(0), 8.0, -BIG, OP.is_ge, OP.mult)
+    ts(col(21), col(21), -SH - 1, None, OP.add)
+    ts(col(13), R("cm", 0, 1), BIG, None, OP.mult)
     bd8 = g8("BD")
-    for buf, n, wgt in (("zb", 2, col(13)), ("zf", 0, col(9)), ("zf", 1, col(11)), ("zf", 2, col(12))):
+    for buf, n, wgt in (("zb", 2, col(13)), ("zf", 0, col(9)), ("zf", 1, R("cm", 5, 6)), ("zf", 2, R("cm", 8, 9))):
         ts(R(buf, 144 * n + 15, 144 * n + 143, 16), bd8, wgt, None, OP.mult)
-    for nm, of, f in (("NI", "I", -1.0), ("IB", "I", BIG), ("NIB", "I", -BIG), ("I4", "I", 4096.0), ("BDH", "BD", 0.5),
+    for k in range(16):
+        ts(SEL(k), M("BD"), R("cm", k, k + 1), None, OP.mult)
+    for nm, of, f in (("NI", "I", -1.0), ("IB", "I", BIG), ("NIB", "I", -BIG), ("I4", "I", 4096.0), ("I3", "I", 3.0), ("BDH", "BD", 0.5),
                       ("NBDH", "BD", -0.5), ("BDB", "BD", BIG), ("NBDB", "BD", -BIG), ("NBD", "BD", -1.0)):
-        ts(M(nm), M(of), f, None, OP.mult)
+        act(M(nm), M(of), AF.Identity, 0.0, f)
     cp(R("b16", 0, 8), bd8)
     cp(R("b16", 8, 16), bd8)
+    ts(R("b16", 16, 32), R("b16", 0, 16), 0.5, None, OP.mult)
     tt(M("S1"), M("S1"), M("S2"), OP.add)
     tt(M("ISH"), M("S1"), M("I"), OP.add)
     cp(IF, M("I"))
     cp(SHF, M("S1"))
-    cp(R("l32", 256, 384), M("BD"))
-    asel(LB, R("l32", 256, 384), [[0, 8], [-1, 16]], OP.is_ge, 0.0, 7, 0, [s_x])
-    asel(LZ, R("l32", 256, 384), [[0, 8], [1, 16]], OP.is_ge, 0.0, -8, 0, [s_x])
+    act(R("l32", 256, 384), M("BD"), AF.Identity)
+    asel(LB, R("l32", 256, 384), [[0, 8], [-1, 16]], OP.is_ge, 0.0, 7, 0, late)
+    asel(LZ, R("l32", 256, 384), [[0, 8], [1, 16]], OP.is_ge, 0.0, -8, 0, late)
     ts(R("om", 0, 384), R("om", 0, 384), 15, None, OP.bitwise_and)
     for t in range(RO):
         ts(M("TR%d" % t), R("om", 128 * t, 128 * t + 128), col(t), BIG, OP.is_gt, OP.mult)
@@ -261,191 +303,250 @@ def build(g, core, T, topo):
     asel(tr3, tr3, [[0, 3], [-16, 8], [0, 16]], OP.is_ge, 0.0, 0, 1)
     asel(tr3, tr3, [[0, 3], [16, 8], [0, 16]], OP.is_ge, 0.0, 15, -1)
     asel(tr3, tr3, [[0, 3], [-1, 128]], OP.not_equal, -BIG, 0, 1)
-    ts(R("dw", 0, 16), R("dw", 0, 16), col(0), None, OP.add)
-
-    ts(R("tab", me, me + V), R("sti", 0, V), -SH, None, OP.add, after=[s_b])
-    ms(R("tab", W, TW), SH)
+    ts(col(19), col(0), 2.0, None, OP.mult)
+    ts(R("dw", 0, 16), R("dw", 0, 16), col(19), None, OP.add)
+    ms(R("tab", W, TW), float(W))
     ms(R("xt", W, W + 16), 0.0)
-    for (lo, hi, nm, sn, lat) in ((0, D2, "sa", s_a, 4500), (D2, DC, "sb", s_b, 7000), (DC, V, "sh", s_h, 9000)):
-        for n, s in enumerate(others):
-            piece = R("lan", V * s + lo, V * s + hi)
-            arrive(piece, "%s%d" % (nm, s), NE, [sn], lat)
-            if nm == "sh":
-                mm([(R("p%d" % (4 + n), 0, HC), IF, piece)])
-                act(R("tab", piece[1], piece[2]), R("p%d" % (4 + n), 0, HC), AF.Identity)
+    soon[0] = None
+    ts(R("w16", 512, 1024), R("w16", 0, 512), 1.0, None, OP.add)
+    iota(R("io2", 0, 512), [[-32, 4], [0, 4], [-1, 32]], 0, 1, late)
+    ts(R("rep", 0, 512), R("io2", 0, 512), 0.0, None, OP.is_equal)
+    for q in range(N):
+        ts(R("pq", 224 * q, 224 * q + 224), R("ones", 0, 224), 0.0, None, OP.mult)
+        cp(R("pq", 224 * q + 96, 224 * q + 128), R("rep", 128 * q, 128 * q + 32))
+
+    soon[0] = DUE["load"]
+    for n, s in enumerate([rank] + ring[-2::-1]):
+        if s != rank:
+            arrive(blk("lan", s), "sa%d" % s, NE, [s_a[n - 1]], 3500)
+        for h in range(2):
+            bank = "p%d" % (2 * (n % 2) + h + 4)
+            mm([(R(bank, 256 * c, 256 * c + 256), blk("un", 2 * h + c, 128), blk("lan", s)) for c in range(2)])
+            to = R("tab", V * s + 512 * h, V * s + 512 * h + 512)
+            if h == 0:
+                act(to, R(bank, 0, 512), AF.Identity, SH)
             else:
-                cp(R("tab", piece[1], piece[2]), piece)
-    for s in others:
-        arrive(R("xt", V * s, V * s + V), "sx%d" % s, NE, [s_x], 18000)
+                ts(to, R(bank, 0, 512), SH, None, OP.add)
+    soon[0] = None
 
     TAB, XT = R("tab", 0, W + 8), R("xt", 0, W + 16)
-    ends = [sum(PCH[:i + 1]) for i in range(len(PCH))]
-    flip = [0, 0]
+    flip, eqs, last, clock = [0, 0, 0], [], [], [0.0]
+
+    def chain(i):
+        for j in last:
+            ops[i]["deps"].setdefault(j, False)
+        last[:] = [due(i, clock[0])]
+        clock[0] += ops[i]["cost"]
+
     for t in range(RO):
         par = t % 2
         base[0] = len(ops)
-        own = lambda a, b: R("tab", me + par + 2 * a, me + 2 * b, 2)
-        o1 = ts(R("so", 0, 64), own(0, 64), SH, None, OP.add)
-        o2 = cp(R("s16", 0, 64), own(0, 64), [o1])
-        cp(R("s16", 64, 512), own(64, 512), [o2])
+        own = lambda a, b: ("ind", TAB, R("ao2", 32 * par + a // 16, 32 * par + b // 16))
+        cp(R("so", 0, 64), own(0, 64))
+        ts(R("s16", 0, 64), R("so", 0, 64), -SH, None, OP.add)
+        ts(R("s16", 64, 512), own(64, 512), -SH, None, OP.add)
         ts(R("so", 64, 512), R("s16", 64, 512), SH, None, OP.add)
         ts(R("non", 0, 512), R("s16", 0, 512), SH, None, OP.is_equal)
-        ms(R("cb", C0 + 4, C0 + 260), SH)
-        v0 = 0
-        for nv in CH:
-            v1 = v0 + nv
-            st = nv // 32
-            dup = 16 // st
-            pc = [i for i in range(len(PCH)) if ends[i] >= v1][0]
-            n = PCH[pc]
-            u0, u1 = ends[pc] - n, ends[pc]
+        for o in range(N):
+            iota(R("cb", C0 + 1 + 512 * o, C0 + 65 + 512 * o), [[0, 64]], 30000, 0)
+        clock[0] = RL * t + DUE["test"]
+        for v0, v1 in parts(CH):
+            st = (v1 - v0) // 32
+            pc, (u0, u1) = [(i, p) for i, p in enumerate(parts(PCH)) if p[1] >= v1][0]
+            n = u1 - u0
             U = lambda b: R(b, u0, u1)
-            act(R("gg", 16 * v0, 16 * v1), ("ind", TAB, R("so", v0, v1)), AF.Identity)
+            act(R("gg", 16 * v0, 16 * v1), ("ind", TAB, R("so", v0, v1)), AF.Identity, -SH)
             if v0 == u0:
                 flip[1] += 1
                 hb = "p%d" % (4 + flip[1] % 2)
                 mm([(R(hb, 0, 128, 1, n), U("non"), M("I")), (R(hb, 128, 256, 1, n), U("non"), M("ISH"))], True, False)
-            mm([(R("p2", d, 512, dup), IF, R("w16", 512 * par + v0, 512 * par + v1)) for d in range(dup)])
-            for kp in range(st):
-                cbk = "p%d" % (flip[0] % 2)
-                flip[0] += 1
-                mm([(R(cbk, d, 512, dup), SEL((st * d + kp + 1) % 16), R("s16", v0, v1)) for d in range(dup)])
-                gs = R("gg", 16 * v0 + kp, 16 * v1, st)
-                for eb, tgt, o in (("e1", "p2", 0), ("e2", cbk, 128)):
-                    tt(R(eb, gs[1], gs[2], st), gs, R(tgt, 0, 512), OP.is_equal)
-                    if v1 == u1:
-                        mm([(R(hb, o + k, o + 128, 16, n), R(eb, 16 * u0 + k, 16 * u1, 16), bd8) for k in range(kp, 16, st)],
-                           False, kp == st - 1 and o > 0)
-            v0 = v1
+            w0, w1 = (v0, v1) if pc == 0 else (u0, u1)
+            sw = (w1 - w0) // 32
+            tests = [("e2", v0, v1, st, kp) for kp in range(st)]
+            if v1 == w1:
+                ws = [("e1", w0, w1, sw, kp) for kp in range(sw)]
+                tests = [x for p in zip(ws, tests) for x in p] + ws[st:]
+            if v0 == w0:
+                mm([(R("p2", d, 512, 16 // sw), IF, R("w16", 512 * par + w0, 512 * par + w1)) for d in range(16 // sw)])
+            for eb, a, b, s, kp in tests:
+                tgt, o = "p2", 0
+                if eb == "e2":
+                    tgt, o = "p%d" % (flip[0] % 2), 128
+                    flip[0] += 1
+                    mm([(R(tgt, d, 512, 16 // s), SEL((s * d + kp + 1) % 16), R("s16", a, b)) for d in range(16 // s)])
+                gs = R("gg", 16 * a + kp, 16 * b, s)
+                chain(tt(R(eb, gs[1], gs[2], s), gs, R(tgt, 0, 512), OP.is_equal))
+                if b == u1:
+                    mm([(R(hb, o + k, o + 128, 16, n), R(eb, 16 * u0 + k, 16 * u1, 16), bd8) for k in range(kp, 16, s)],
+                       False, (eb, a, b, s, kp) == tests[-1])
             if v1 != u1:
                 continue
-            boost[0] = BOOST
             t1, t2, t3 = R("p6", 0, n), R("p6", n, 2 * n), R("p6", 2 * n, 3 * n)
             tr = M("TR%d" % t)
             s1, s2 = R("sg", 256 * pc, 256 * pc + 128, 1, n), R("sg", 256 * pc + 128, 256 * pc + 256, 1, n)
             a1, ok = R("ao", 2 * u0, 2 * u0 + n), R("ao", 2 * u0 + n, 2 * u1)
             act(R("sg", 256 * pc, 256 * pc + 256, 1, n), R(hb, 0, 256, 1, n), AF.Sign)
-            idn = R("mb", M("I")[1], M("I")[1] + n, 1, n)
             b1, b2 = R(hb, 256, 256 + n), R(hb, 256 + n, 256 + 2 * n)
-            mm([(b2, M("NI"), R("ones", 0, n)), (b1, s1, idn), (b2, s1, idn), (b2, s2, idn)])
-            act(R("ao", 2 * u0, 2 * u1), R(hb, 256, 256 + 2 * n), AF.Relu)
-            mm([(t1, IF, U("s16")), (t2, SHF, U("s16")), (t3, IF, R("w16", 512 * par + u0, 512 * par + u1)),
-                (t2, M("NIB"), R("ones", 0, n))], True, False)
+            mm([(b1, s1, M("I3", n)), (b2, s1, M("I", n)), (b2, s2, M("I", n))])
+            act(R("ao", 2 * u0, 2 * u1), R(hb, 256, 256 + 2 * n), AF.Sign, -1.5)
+            mm([(t1, IF, U("s16")), (t2, SHF, U("s16")), (t3, IF, R("w16", 512 * par + u0, 512 * par + u1))], True, False)
             mm([(t2, M("IB"), a1), (t3, M("NIB"), a1), (t1, tr, ok), (t2, tr, ok), (t3, tr, ok)], False, True)
             rr = lambda a, b: R("rr", 3 * u0 + a * n, 3 * u0 + b * n)
             act(rr(0, 3), R("p6", 0, 3 * n), AF.Relu, col(4 + t))
             bz = R("p7", 0, n)
             mm([(bz, LB, rr(0, 1)), (bz, LZ, rr(1, 2)), (bz, LZ, rr(2, 3))])
-            act(U("ab"), bz, AF.Abs, col(10))
-            act(U("bzs"), bz, AF.Identity, -SH - 1)
-            ts(U("ind"), U("ab"), 512.0, None, OP.is_lt)
-            scan(U("val"), U("ind"), U("ind"), col(7) if u0 == 0 else R("val", u0 - 1, u0), OP.add, OP.max)
-            scan(U("prod"), U("val"), U("ind"), 0.0, OP.max, OP.mult)
-            ob = R("p3", 0, n // 16)
-            mm([(ob, Z("zf", 0, a), R("prod", u0 + a, u1, 16)) for a in range(16)])
-            ts(R("co", u0 // 16, u1 // 16), ob, float(C0), None, OP.add)
-            scat(R("cb", 0, 2576), R("co", u0 // 16, u1 // 16), U("bzs"))
-            boost[0] = 0.0
+            due(act(U("ab"), bz, AF.Abs, col(10)), RL * t + DUE["sel"][pc])
+            for u0, u1 in [p for p in parts(VCH) if p[1] == u1]:
+                ts(U("ind"), U("ab"), 512.0, None, OP.is_lt)
+                scan(U("val"), U("ind"), U("ind"), col(7) if u0 == 0 else col(20), OP.add, OP.max)
+                scan(U("prod"), U("val"), U("ind"), 0.0, OP.max, OP.mult)
+                if u1 < 512:
+                    cp(col(20), R("val", u1 - 1, u1))
+                ob = R("p3", 0, (u1 - u0) // 16)
+                mm([(ob, Z("zf", 0, a), R("prod", u0 + a, u1, 16)) for a in range(16)])
+                ts(R("co", u0 // 16, u1 // 16), ob, float(C0), None, OP.add)
+                due(scat(R("cb", 0, 2576), R("co", u0 // 16, u1 // 16), U("ab")), RL * t + DUE["pack"][u1 // 512])
         for o in range(N):
-            cp(R("c16", 64 + 64 * o, 128 + 64 * o), R("cb", C0 + 4 + o, C0 + 260, 4))
-        mm([(R("p7", 0, 16), Z("zf", 1, a), R("c16", 64 + a, 320, 16)) for a in range(16)])
+            ts(R("c16", 64 + 64 * o, 128 + 64 * o), R("cb", C0 + 1 + 512 * o, C0 + 65 + 512 * o), col(21), SH, OP.add, OP.min)
+            if o == 0:
+                mm([(R("p7", 0, 4), Z("zf", 1, a), R("c16", 64 + a, 128, 16)) for a in range(16)])
+                ts(R("obz", 0, 4), R("p7", 0, 4), SH, None, OP.add)
+                cp(R("eo", 0, 64), ("ind", TAB, R("obz", 0, 4)))
+                cp(R("xbz", 0, 64), ("ind", XT, R("obz", 0, 4)))
         mm([(R("p3", 0, 16), Z("zf", 2, a), R("c16", 64 + a, 320, 16)) for a in range(16)])
-        ts(R("obz", 0, 16), R("p7", 0, 16), SH, None, OP.add)
-        for lo, hi in ((0, 64), (64, 256)):
-            ts(R("eo", lo, hi), ("ind", TAB, R("obz", lo // 16, hi // 16)), SH, None, OP.add)
         ts(R("obz", 16, 32), R("p3", 0, 16), SH, None, OP.add)
-        for o in (256, 0):
-            cp(R("xbz", o, o + 128), ("ind", XT, R("obz", o // 16, o // 16 + 8)))
-        boost[0] = DB
-        mm([(R("p3", 0, 256), SEL(0), R("c16", 64, 320))])
-        act(R("bbs", 0, 256), R("p3", 0, 256), AF.Identity)
-        act(R("inv", 0, 256), R("p3", 0, 256), AF.Relu, 1.0 - SH)
-        for q in range(4):
-            mm([(R("p1", 0, 304), Z("zf", 1, a), R("c16", 15 - a, 319 - a)) for a in range(4 * q, 4 * q + 4)], q == 0, q == 3)
-        for q in range(4):
-            tt(R("eq", 256 * q, 256 * q + 256), R("bbs", 0, 256), R("p1", 48 - 16 * q, 304 - 16 * q), OP.is_equal)
-        mm([(R("p3", 0, 256), M("I"), R("inv", 0, 256))] + [(R("p3", 0, 256), M("BD"), R("eq", 256 * q, 256 * q + 256)) for q in range(4)])
-        act(R("cnt", 0, 256), R("p3", 0, 256), AF.Identity)
-        mm([(R("p1", 0, 16), Z("zf", 1, a), R("c16", 64 + a, 320, 16)) for a in range(16)], True, False)
-        mm([(R("p1", 0, 16), Z("zb", 2, a), R("cnt", a, 256, 16)) for a in range(16)], False, True)
-        boost[0] = BOOST
+        cp(R("xbz", 256, 320), ("ind", XT, R("obz", 16, 20)))
+        mm([(R("p7", 4, 16), Z("zf", 1, a), R("c16", 128 + a, 320, 16)) for a in range(16)])
+        ts(R("obz", 4, 16), R("p7", 4, 16), SH, None, OP.add)
+        cp(R("eo", 64, 256), ("ind", TAB, R("obz", 4, 16)))
+        cp(R("xbz", 64, 256), ("ind", XT, R("obz", 4, 16)))
+        cp(R("xbz", 320, 512), ("ind", XT, R("obz", 20, 32)))
+        ts(R("sbf", 0, 256), R("eo", 0, 256), -SH, None, OP.add)
+        ts(R("nj", 0, 256), R("eo", 0, 256), float(W), None, OP.is_equal)
+        mm([(R("p3", 0, 256), M("I"), R("xbz", 256, 512)), (R("p3", 0, 256), M("NI"), R("xbz", 0, 256))])
+        act(R("dzb", 0, 256), R("p3", 0, 256), AF.Abs)
+        for a in range(16):
+            dma("s", T.shf[a:128:16, 0:304], T.c16[5:128:16, 15 - a:319 - a], [R("c16", 15 - a, 319 - a)], [], "sf", 2500, eqs)
+        landed(R("shf", 0, 304), "sf")
+        mm([(R("p1", 0, 256), SEL(5), R("c16", 64, 320))])
+        eqs = [tt(R("eq", 256 * q, 256 * q + 256), R("shf", 48 - 16 * q, 304 - 16 * q), R("p1", 0, 256), OP.is_equal) for q in range(4)]
+        mm([(R("p1", 0, 256), M("BD"), R("eq", 256 * q, 256 * q + 256)) for q in range(4)])
+        act(R("cnt", 0, 256), R("p1", 0, 256), AF.Identity)
+        ts(R("bl", 0, 16), R("obz", 0, 16), -SH, None, OP.add)
+        mm([(R("p1", 0, 16), IF, R("bl", 0, 16))] + [(R("p1", 0, 16), Z("zb", 2, a), R("cnt", a, 256, 16)) for a in range(16)])
         tt(R("tg", 0, 16), R("dw", 0, 16), R("p1", 0, 16), OP.min)
-        mo = lambda s: 64 * t + 16 * s
-        md = lambda s: 1024 * t + 256 * s
-        ts(R("mo", mo(rank), mo(rank) + 16), R("tg", 0, 16), SH, None, OP.add)
-        s_o = send([(R("mo", mo(rank), mo(rank) + 16), peers)], "mo%d%d" % (t, rank), off_eng)
-        boost[0] = 0.0
-        for s in others:
-            arrive(R("mo", mo(s), mo(s) + 16), "mo%d%d" % (t, s), NE, [s_o], 3000)
-        last, sent = [], []
-        for h in range(2):
-            s0 = 128 * h
-            H = lambda b, o=0: R(b, o + s0, o + s0 + 128)
-            K = lambda b, k: R(b, 16 * s0 + k, 16 * s0 + 2048, 16)
-            hb = "p%d" % (4 + h)
-            r2, r1 = R(hb, 0, 128), R(hb, 128, 256)
-            for q in range(2):
-                c0 = s0 + 64 * q
-                act(R("xe", 16 * c0, 16 * c0 + 1024), ("ind", XT, R("eo", c0, c0 + 64)), AF.Identity)
-                if q == 0:
-                    if h == 1:
-                        for o in (384, 128):
-                            act(R("xbz", o, o + 128), ("ind", XT, R("obz", o // 16, o // 16 + 8)), AF.Identity)
-                    act(H("sbf"), ("ind", TAB, R("obz", 8 * h, 8 * h + 8)), AF.Identity)
-                    act(H("nj"), H("sbf"), AF.Relu, 1.0 - SH)
-                    mm([(R("p7", 0, 128), M("I"), H("xbz", 256)), (R("p7", 0, 128), M("NI"), H("xbz"))])
-                    act(H("dzb"), R("p7", 0, 128), AF.Abs)
-                mm([(R("p0", d, 512, 8), M("I"), R("xbz", 256 + c0, 320 + c0)) for d in range(8)])
-                mm([(R("p2", d, 512, 8), M("I"), R("xbz", c0, c0 + 64)) for d in range(8)])
-                if q == 1:
-                    mm([(r2, H("nj"), M("IB")), (r1, H("nj"), M("IB")), (r2, H("xbz", 256), M("NBDH")), (r2, H("xbz"), M("BDH")),
-                        (r1, H("xbz", 256), M("NBDH")), (r1, H("dzb"), M("NBDH"))], True, False)
-                    for kp in range(2):
-                        mm([(R(hb, 128 + k, 256, 16), K("xe", k), g8("NBDH")) for k in range(kp, 16, 2)], False, False)
+        if t < RO - 1:
+            mm([(R("p1", 256 + 16 * s, 272 + 16 * s), blk("rep", s, 128), R("tg", 0, 16)) for s in range(N)])
+            ts(R("mo", 0, 64), R("p1", 256, 320), SH, None, OP.add)
+        else:
+            s_o = send([(R("tg", 0, 16), blk("lt", rank, 16), peers)], "lt%d" % rank, off_eng)[0]
+        due(len(ops) - 1, RL * t + DUE["mo"])
+        sent = {}
+        clock[0] = RL * t + DUE["max"]
+        for c0, c1 in parts(SUB):
+            st = (c1 - c0) // 32
+            dup = 16 // st
+            h, (s0, s1) = [(i, p) for i, p in enumerate(parts(JC[t])) if p[1] >= c1][0]
+            n = s1 - s0
+            H = lambda b, o=0: R(b, o + s0, o + s1)
+            K = lambda b, k: R(b, 16 * s0 + k, 16 * s1, 16)
+            hb = "p%d" % (4 + h % 2)
+            r2, r1 = R(hb, 0, 128, 1, n), R(hb, 128, 256, 1, n)
+            act(R("xe", 16 * c0, 16 * c1), ("ind", XT, R("eo", c0, c1)), AF.Identity)
+            mm([(R("p2", d, 512, dup), M("I"), R("xbz", c0, c1)) for d in range(dup)])
+            byv = [kp for kp in range(2) if (h, kp) not in ABS[t]]
+            if byv:
+                mm([(R("p0", d, 512, dup), M("I"), R("xbz", 256 + c0, 256 + c1)) for d in range(dup)])
+            if c1 == s1:
+                odd = lambda r, kp: R(r[0], r[1] + kp, r[2], 2, r[4])
+                mm([(r2, H("nj"), M("IB")), (r1, H("nj"), M("IB")), (r2, H("xbz"), M("BDH")), (r1, H("dzb"), M("NBDH"))] +
+                   [(odd(r, kp), H("xbz", 256), odd(M("NBDH"), kp)) for kp in byv for r in (r1, r2)], True, False)
                 for kp in range(2):
-                    xs = R("xe", 16 * c0 + kp, 16 * c0 + 1024, 2)
-                    for eb, tgt, hi, w8 in (("e1", "p0", 256, R("b16", 0, 16)), ("e2", "p2", 128, g8("NBD"))):
-                        tt(R(eb, xs[1], xs[2], 2), xs, R(tgt, 0, 512), OP.max)
-                        if q == 1:
-                            mm([(R(hb, k, hi, 16), K(eb, k), w8) for k in range(kp, 16, 2)], False, kp == 1 and eb == "e2")
-            boost[0] = BOOST
-            pu, px = R("p6", 0, 128), R("p6", 128, 256)
-            mm([(pu, M("I4"), R("mhalf", 0, 128)), (px, SEL(8), H("c16", 64)), (px, M("IB"), R("ones", 0, 128)), (px, M("TR0"), H("nj"))], True, False)
-            f0 = 2 * s0
-            ev, rf = R("er", f0, f0 + 128), R("er", f0 + 128, f0 + 256)
-            act(R("fl", f0, f0 + 256), R(hb, 0, 256), AF.Sign)
-            mm([(R(hb, 256, 384), R("fl", f0, f0 + 128), M("NI")), (R(hb, 384, 512), R("fl", f0 + 128, f0 + 256), M("NI"))])
-            act(R("er", f0, f0 + 256), R(hb, 256, 512), AF.Relu)
+                    o, w8 = (128, g8("NBDH")) if kp in byv else (0, g8("BDH"))
+                    mm([(R(hb, o + k, o + 128, 16, n), K("xe", k), w8) for k in range(kp, 16, 2)], False, False)
+            items = [(kp, eb) for kp in range(st) for eb in ("e2", "e1")]
+            items = [x for x in items if x[1] == "e2" or x[0] in byv] + [x for x in items if x[1] == "e1" and x[0] not in byv]
+            for kp, eb in items:
+                xs = R("xe", 16 * c0 + kp, 16 * c1, st)
+                tgt, hi, w8 = ("p2", 128, g8("NBD")) if eb == "e2" else ("p0", 256, R("b16", 0, 16))
+                if eb == "e1" and kp not in byv:
+                    bank = "p%d" % (3 + 4 * (flip[2] % 2))
+                    flip[2] += 1
+                    mm([(R(bank, 0, 512), M("I"), xs)] + [(R(bank, d, 512, dup), M("NI"), R("xbz", 256 + c0, 256 + c1)) for d in range(dup)])
+                    due(act(R(eb, xs[1], xs[2], st), R(bank, 0, 512), AF.Abs), clock[0] + DUE["abs"])
+                    w8 = R("b16", 16, 32)
+                else:
+                    chain(tt(R(eb, xs[1], xs[2], st), xs, R(tgt, 0, 512), OP.max))
+                if c1 == s1:
+                    mm([(R(hb, k, hi, 16, n), K(eb, k), w8) for k in range(kp, 16, st)], False, (kp, eb) == items[-1])
+            if c1 != s1:
+                continue
+            pu, px = R("p6", 0, n), R("p6", 128, 128 + n)
+            mm([(pu, M("I4"), R("mhalf", 0, n)), (px, SEL(8), H("c16", 64)), (px, M("IB"), R("ones", 0, n)), (px, M("TR0"), H("nj"))], True, False)
+            ev, rf = R("er", 2 * s0, 2 * s0 + n), R("er", 2 * s0 + n, 2 * s1)
+            act(R("fl", 256 * h, 256 * h + 256, 1, n), R(hb, 0, 256, 1, n), AF.Sign)
+            mm([(R(hb, 256 + n * i, 256 + n * i + n), R("fl", 256 * h + 128 * i, 256 * h + 128 * i + 128, 1, n), M("NI", n)) for i in range(2)])
+            act(R("er", 2 * s0, 2 * s1), R(hb, 256, 256 + 2 * n), AF.Relu)
             mm([(pu, M("NBDB"), rf), (px, M("BDB"), rf), (pu, M("I4"), ev), (px, M("TR0"), ev)], False, True)
             tt(H("uu"), H("sbf"), pu, OP.max)
-            last.append(tt(H("md", md(rank)), H("uu"), px, OP.min))
-            sem = "md%d%d%d" % (t, h, rank)
+            due(tt(H("md"), H("uu"), px, OP.min), RL * t + DUE["md"][h if s1 < 256 else 2])
             if t < RO - 1:
-                sent.append(send([(H("md", md(rank)), peers)], sem, off_eng))
+                got = lambda s, k=1: R("mf32", 4 * s0 + n * s, 4 * s0 + n * (s + k))
+                mm([(R("p1", n * s, n * s + n), blk("rep", s, 128), H("md")) for s in range(N)])
+                act(got(2, 2), R("p1", 2 * n, 4 * n), AF.Identity, SH)
+                act(got(0, 2), R("p1", 0, 2 * n), AF.Identity, SH)
+                for s in range(N - 1, -1, -1):
+                    due(scat(R("tab", 0, TW), R("mo", 16 * s + s0 // 16, 16 * s + s1 // 16), got(s)), RL * t + DUE["tab"][h])
             else:
-                sent.append(send([(R("md", md(rank) + 64 * o, md(rank) + 64 * o + 64), [T.cores[o]]) for o in (2 * h, 2 * h + 1) if o != rank],
-                                 sem, off_eng))
-            boost[0] = 0.0
-        for h in range(2):
-            if t == RO - 1 and h != rank // 2:
-                continue
-            lo, n = (128 * h, 128) if t < RO - 1 else (64 * rank, 64)
-            for s in range(N - 1, -1, -1):
-                dat = R("md", md(s) + lo, md(s) + lo + n)
-                if s != rank:
-                    arrive(dat, "md%d%d%d" % (t, h, s), NE if t < RO - 1 or s // 2 == h else NE // 2, [sent[h]], 3500)
-                scat(R("tab", 0, TW), R("mo", mo(s) + lo // 16, mo(s) + (lo + n) // 16), dat, [last[1]])
-    act(R("yb", 0, 512), R("tab", me, me + 512), AF.Identity, SH)
-    ts(R("yb", 512, V), R("tab", me + 512, me + V), SH, None, OP.add)
-    add("a", lambda: g.scalar.dma_start(T.y[:, 0:512], T.yb[:, 0:512]), 50, [R("yb", 0, 512)], [], sem="st0", val=16, lat=2500)
-    add("s", lambda: g.sync.dma_start(T.y[:, 512:V], T.yb[:, 512:V]), 50, [R("yb", 512, V)], [], sem="st1", val=16, lat=2500)
+                to = [j for j in range(s0 // 64, s1 // 64) if ring[j] != rank]
+                if to:
+                    out = send([(blk("md", j, 64), blk("lm", rank, 64), [T.cores[ring[j]]]) for j in to], "lm%d" % rank, off_eng)
+                    sent.update({j: out for j in to})
+        if t == RO - 2:
+            for d in ring[:-1]:
+                dma("s", ap(blk("stg", d)), T.tab[rows(0), V * d:V * d + V], [R("tab", V * d, V * d + V)], [blk("stg", d)], "sg%d" % d, 3000)
+            s_y, ky = send([(blk("stg", d), blk("ls", rank), [T.cores[d]]) for d in ring[:-1]], "sy%d" % rank, off_eng)
+            for s in ring[::-1]:
+                if s == rank:
+                    dma("s", T.yb[rows(s), 0:V], T.tab[rows(0), V * s:V * s + V], [R("tab", V * s, V * s + V)], [], "yb", 3000)
+                else:
+                    arrive(blk("ls", s), "sy%d" % s, ky, [s_y], 9000)
+                    dma("s", T.yb[rows(s), 0:V], ap(blk("ls", s)), [blk("ls", s)], [], "yb", 3000)
+            due(landed(R("yb", 0, V), "yb"), RL * (RO - 1) + DUE["test"] + 15000)
+    terms = []
+    for s in ring:
+        j = 4 * ((rank - s - 1) % N)
+        if s != rank:
+            arrive(blk("lt", s, 16), "lt%d" % s, NE, [s_o], 3000)
+        got = R("lt", 16 * s + j, 16 * s + j + 4) if s != rank else R("tg", j, j + 4)
+        terms += [(R("p1", 256 + 4 * q, 260 + 4 * q), PQ(s, q), got) for q in range(N)]
+    mm(terms)
+    ts(R("mo", 0, 16), R("p1", 256, 272), SH - V * rank, None, OP.add)
+    for s in ring[-2::-1] + [rank]:
+        j = (rank - s - 1) % N
+        if s != rank:
+            arrive(blk("lm", s, 64), "lm%d" % s, sent[j][1], [sent[j][0]], 3500)
+        got = blk("lm", s, 64) if s != rank else blk("md", j, 64)
+        mm([(blk("p1", q, 64), PQ(s, q), got) for q in range(N)], j == 0, s == rank)
+    act(R("mf32", 128, 256), R("p1", 128, 256), AF.Identity, SH)
+    act(R("mf32", 0, 128), R("p1", 0, 128), AF.Identity, SH)
+    for q in range(N - 1, -1, -1):
+        scat(R("yb", 0, TW), blk("mo", q, 4), blk("mf32", q, 64))
+    dma("a", T.y[:, 0:512], T.yb[:, 0:512], [R("yb", 0, 512)], [], "st0", 2500)
+    dma("s", T.y[:, 512:V], T.yb[:, 512:V], [R("yb", 512, V)], [], "st1", 2500)
     return ops, Q, nloc[0]
 
 
-def order(ops, kids, pr, noise):
+def plan(ops):
     n = len(ops)
+    kids = [[] for _ in range(n)]
+    for i, o in enumerate(ops):
+        for j in o["deps"]:
+            kids[j].append(i)
+    key = [0.0] * n
+    for i in range(n - 1, -1, -1):
+        key[i] = min([ops[i]["due"]] + [key[k] - HOP - ops[i]["cost"] - max(ops[i]["lat"], 0.0) for k in kids[i]])
     left = [len(o["deps"]) for o in ops]
-    key = [pr[i] + ops[i]["boost"] + noise.get(ops[i]["tag"], 0.0) for i in range(n)]
     rdy = [0.0] * n
     pool = {e: [] for e in "vapgsx"}
     free = {e: 0.0 for e in "vapgsx"}
@@ -454,14 +555,8 @@ def order(ops, kids, pr, noise):
             pool[ops[i]["eng"]].append(i)
     seq = []
     while len(seq) < n:
-        best = None
-        for e in pool:
-            if pool[e]:
-                t0 = max(free[e], min(rdy[i] for i in pool[e]))
-                if best is None or t0 < best[0]:
-                    best = (t0, e)
-        t0, e = best
-        i = max([i for i in pool[e] if rdy[i] <= t0 + LOOK], key=lambda i: key[i])
+        t0, e = min((max(free[e], min(rdy[i] for i in pool[e])), e) for e in pool if pool[e])
+        i = min([i for i in pool[e] if rdy[i] <= t0 + LOOK], key=lambda i: key[i])
         pool[e].remove(i)
         t0 = max(t0, rdy[i])
         if e != "x":
@@ -474,48 +569,6 @@ def order(ops, kids, pr, noise):
             if left[k] == 0:
                 pool[ops[k]["eng"]].append(k)
     return seq
-
-
-def span(ops, seq, pe, ga, hop):
-    done = [0.0] * len(ops)
-    free = {e: 0.0 for e in "vapgsx"}
-    for i in seq:
-        o = ops[i]
-        t0 = max([free[o["eng"]]] + [done[j] + (hop if h else 0.0) for j, h in o["deps"].items()])
-        c = o["cost"] * (pe if o["pe"] else 1.0) + CYC * (ga - GA) * o["ga"]
-        if o["eng"] != "x":
-            free[o["eng"]] = t0 + c
-        done[i] = t0 + c + max(o["lat"], 0.0)
-    return max(done), done
-
-
-FOUND = {}
-
-
-def plan(ops):
-    n = len(ops)
-    kids = [[] for _ in range(n)]
-    for i, o in enumerate(ops):
-        for j in o["deps"]:
-            kids[j].append(i)
-    pr = [0.0] * n
-    for i in range(n - 1, -1, -1):
-        pr[i] = ops[i]["cost"] + max(ops[i]["lat"], 0.0) + max([pr[k] + HOP for k in kids[i]] + [0.0])
-    score = lambda q: sum(span(ops, q, *f)[0] for f in FIGS)
-    if "noise" not in FOUND:
-        rng = np.random.default_rng(1)
-        tags = sorted(set(o["tag"] for o in ops))
-        noise = {}
-        best = score(order(ops, kids, pr, noise))
-        for _ in range(TRIES):
-            cand = dict(noise)
-            for k in rng.choice(len(tags), 6):
-                cand[tags[int(k)]] = float(rng.normal()) * float(rng.choice([1000.0, 5000.0, 30000.0]))
-            val = score(order(ops, kids, pr, cand))
-            if val <= best:
-                best, noise = val, cand
-        FOUND["noise"] = noise
-    return order(ops, kids, pr, FOUND["noise"])
 
 
 def emit(g, T, ops, Q, nloc):
@@ -558,12 +611,3 @@ def rank_program(g, core, T, topo):
     if T.rank_of(core) is not None:
         ops, Q, nloc = build(g, core, T, topo)
         emit(g, T, ops, Q, nloc)
-        return
-    for rank, c in enumerate(T.cores):
-        peers = [p for p in T.cores if p != c]
-        if helper_of(c, peers, topo) == core:
-            own = common_engines(c, peers, topo)
-            eng = common_engines(core, peers, topo)
-            g.wait_ge(T.sem.hin, len([e for e in topo.engines(c, core) if e not in own]))
-            g.remote_dma_fused([transfer(topo, peers, T.lan[:, V * rank + V - HC:V * rank + V], T.sem["sh%d" % rank], eng)], local_sem=T.sem.loc)
-            g.wait_ge(T.sem.loc, len(eng))

@@ -1,9 +1,11 @@
+import numpy as np
 from concourse.bass import DstId, RemoteDMATransfer
 from concourse.mybir import AluOpType as OP, ActivationFunctionType as AF
 
 N, V, W, RO = 4, 1024, 4096, 3
 SH = 2048.0
 BIG = 8192.0
+KZ = (1 - SH + BIG) / 2
 TW = W + 8 + 512
 C0 = 520
 CH = [32, 32] + [64] * 7
@@ -11,21 +13,24 @@ PCH = [128, 128, 128, 128]
 VCH = [384, 128]
 SUB = [64, 64, 64, 64]
 JC = [[128, 128], [128, 128], [128, 64, 64]]
-ABS = [[(1, 1)], [(1, 1)], []]
+ABS = [[(1, 1)], [(1, 1)], [(2, 1)]]
+XV = 128
+SPREAD = [("p2", "p0"), ("p7", "p3")]
 CYC, PEC, GA, SC, HOP, LOOK = 0.83, 0.42, 1.56, 3.8, 100.0, 100.0
-RL = 60000.0
-DUE = {"test": 1700, "sel": [1300, 11400, 12100, 17500], "pack": [30300, 31700], "mo": 30300, "max": 25400, "abs": -2900,
-       "md": [29400, 31000, 44100], "tab": [42300, 36300], "const": -2300, "load": -19500}
-MATS = ["I", "NI", "IB", "NIB", "ISH", "BDH", "NBDH", "BDB", "NBDB", "I4", "TR0", "TR1", "TR2", "BD", "S1", "S2", "NBD", "I3"]
+FIGS = ((1.0, 1.56, 100.0), (0.85, 1.15, 160.0), (1.15, 2.0, 60.0))
+RL, TRIES = 60000.0, 1400
+DUE = {"test": 1500, "sel": [-1700, 11600, 11900, 17500], "pack": [30300, 31700], "mo": 30700, "max": 29400, "abs": -5900,
+       "md": [26400, 31500, 44100], "tab": [41800, 39100], "xbz": 24000, "xe": 27000, "const": -2300, "load": -19500}
+MATS = ["I", "NI", "IB", "ISH", "BDH", "NBDH", "BDB", "NBDB", "I4", "TR0", "TR1", "TR2", "BD", "S1", "S2", "NBD", "I3"]
 F, B, H16, U16, I32 = "float32", "bfloat16", "float16", "uint16", "int32"
 SCRATCH = {n: ("sbuf", [128, w], d) for n, w, d in [
     ("sti", V, I32), ("out", V, H16), ("lan", V, H16), ("xs", V, B), ("xl", V, B), ("io1", 512, B), ("io2", 512, B), ("un", 512, H16),
     ("rep", 512, H16), ("pq", 896, H16), ("cm", 16, F), ("ai", 64, I32), ("ao2", 64, U16), ("stg", V, F), ("ls", V, F), ("mf32", 1024, F),
     ("lm", 256, H16), ("lt", 64, H16), ("tab", TW, F), ("xt", W + 16, B), ("gg", 8192, F), ("e1", 8192, B), ("e2", 8192, B),
-    ("xe", 4096, B), ("mb", 128 * len(MATS), B), ("sel", 2048, H16), ("mf", 256, H16), ("l32", 384, F), ("zb", 432, B),
+    ("xe", 4096, B), ("mb", 128 * len(MATS), B), ("sel", 2048, H16), ("mf", 384, H16), ("l32", 512, F), ("zb", 144, B),
     ("zf", 432, H16), ("ones", 256, B), ("mhalf", 128, B), ("cc", 24, F), ("ci", 8, I32), ("om", 384, I32), ("wf", 512, F),
     ("w16", 1024, H16), ("dw", 16, F), ("s16", 512, H16), ("so", 512, U16), ("non", 512, B), ("sg", 1536, B), ("ao", 1024, B),
-    ("b16", 32, B), ("rr", 1536, F), ("ab", 512, F), ("ind", 512, H16), ("val", 512, H16), ("prod", 512, H16),
+    ("b16", 32, B), ("rr", 1024, F), ("ab", 512, F), ("ind", 512, H16), ("val", 512, H16), ("prod", 512, H16),
     ("co", 32, U16), ("cb", 2576, F), ("c16", 320, H16), ("obz", 32, U16), ("eo", 256, U16), ("xbz", 512, B), ("sbf", 256, H16),
     ("nj", 256, B), ("dzb", 256, B), ("fl", 768, B), ("er", 512, B), ("uu", 256, H16), ("shf", 304, H16), ("bl", 16, H16),
     ("eq", 1024, B), ("cnt", 256, B), ("tg", 16, H16), ("md", 256, H16), ("mo", 64, U16), ("yb", TW, F)]}
@@ -210,7 +215,7 @@ def build(g, core, T, topo):
     def col(k):
         return R("cc", k, k + 1)
 
-    IF, SHF = R("mf", 0, 128), R("mf", 128, 256)
+    IF, SHF, IZ = R("mf", 0, 128), R("mf", 128, 256), R("mf", 256, 384)
     LB, LZ = R("l32", 0, 128), R("l32", 128, 256)
     ring = [(rank + 1 + j) % N for j in range(N)]
     blk = lambda b, d, n=256: R(b, n * d, n * d + n)
@@ -238,10 +243,7 @@ def build(g, core, T, topo):
     landed(R("xt", 0, W), "xt")
 
     ms(R("ones", 0, 256), 1.0)
-    ms(R("mhalf", 0, 128), -0.5)
-    ms(R("zb", 0, 432), 0.0)
-    ts(R("zf", 0, 432), R("zb", 0, 432), 0.0, None, OP.mult)
-    ts(R("c16", 0, 64), R("ones", 0, 64), -3000.0, None, OP.mult)
+    ts(R("zf", 0, 144), R("ones", 0, 144), 0.0, None, OP.mult)
     iota(R("ci", 0, 8), [[0, 2], [-5, 4]], 32, 1)
     iota(R("io1", 0, 512), [[-1, 4], [0, 4], [-4, 32]], 0, 1)
     ts(R("un", 0, 512), R("io1", 0, 512), 0.0, None, OP.is_equal)
@@ -253,7 +255,6 @@ def build(g, core, T, topo):
     asel(M("S2"), M("BD"), [[-1, 128]], OP.is_equal, 0.0, 15, 1, late)
     iota(R("wf", 0, 512), [[2, 512]], -int(SH), 0, late)
     iota(R("ai", 0, 64), [[1, 2], [32, 32]], 0, 0, late)
-    iota(R("om", 0, 384), [[-5, 3], [0, 8], [1, 16]], 32, 0, late)
     iota(R("dw", 0, 16), [[32, 16]], W + 8 - int(SH), 0, late)
     iota(R("cm", 0, 16), [[1, 16]], 0, 0)
     ts(R("ci", 5, 6), R("ci", 4, 5), rank + 1, None, OP.add)
@@ -269,45 +270,55 @@ def build(g, core, T, topo):
     ts(col(9), col(14), col(8), None, OP.subtract)
     ts(col(10), col(17), -1024.0, -512.5, OP.mult, OP.add)
     ts(col(10), col(10), col(14), None, OP.mult)
+    ts(col(22), col(0), 8.0, None, OP.is_ge)
+    ts(col(10), col(22), SH + KZ, col(10), OP.mult, OP.add)
+    ts(IZ, M("I"), col(22), None, OP.mult)
     ts(col(10), col(8), 511.5, col(10), OP.mult, OP.add)
     ts(col(16), col(16), 1024.0, -1024.0, OP.mult, OP.add)
     ts(R("w16", 0, 512), R("wf", 0, 512), col(16), None, OP.add)
     ts(col(18), col(0), 2.0, col(16), OP.mult, OP.add)
     ts(R("ao2", 0, 64), R("ai", 0, 64), col(18), None, OP.add)
     ts(R("cm", 0, 16), R("cm", 0, 16), col(0), None, OP.is_equal)
-    ts(col(21), col(0), 8.0, -BIG, OP.is_ge, OP.mult)
-    ts(col(21), col(21), -SH - 1, None, OP.add)
-    ts(col(13), R("cm", 0, 1), BIG, None, OP.mult)
     bd8 = g8("BD")
-    for buf, n, wgt in (("zb", 2, col(13)), ("zf", 0, col(9)), ("zf", 1, R("cm", 5, 6)), ("zf", 2, R("cm", 8, 9))):
-        ts(R(buf, 144 * n + 15, 144 * n + 143, 16), bd8, wgt, None, OP.mult)
+    ts(R("zf", 15, 143, 16), bd8, col(9), None, OP.mult)
     for k in range(16):
         ts(SEL(k), M("BD"), R("cm", k, k + 1), None, OP.mult)
-    for nm, of, f in (("NI", "I", -1.0), ("IB", "I", BIG), ("NIB", "I", -BIG), ("I4", "I", 4096.0), ("I3", "I", 3.0), ("BDH", "BD", 0.5),
+    for nm, of, f in (("NI", "I", -1.0), ("IB", "I", BIG), ("I4", "I", 4096.0), ("I3", "I", 3.0), ("BDH", "BD", 0.5),
                       ("NBDH", "BD", -0.5), ("BDB", "BD", BIG), ("NBDB", "BD", -BIG), ("NBD", "BD", -1.0)):
         act(M(nm), M(of), AF.Identity, 0.0, f)
-    cp(R("b16", 0, 8), bd8)
-    cp(R("b16", 8, 16), bd8)
-    ts(R("b16", 16, 32), R("b16", 0, 16), 0.5, None, OP.mult)
-    tt(M("S1"), M("S1"), M("S2"), OP.add)
-    tt(M("ISH"), M("S1"), M("I"), OP.add)
+    mm([(R("p0", 0, 128), M("I"), M("S1")), (R("p0", 0, 128), M("I"), M("S2"))] + [(R("p0", 128, 256), M("I"), M(x)) for x in ("S1", "S2", "I")])
+    act(M("ISH"), R("p0", 128, 256), AF.Identity)
+    cp(SHF, R("p0", 0, 128))
     cp(IF, M("I"))
-    cp(SHF, M("S1"))
     act(R("l32", 256, 384), M("BD"), AF.Identity)
     asel(LB, R("l32", 256, 384), [[0, 8], [-1, 16]], OP.is_ge, 0.0, 7, 0, late)
-    asel(LZ, R("l32", 256, 384), [[0, 8], [1, 16]], OP.is_ge, 0.0, -8, 0, late)
-    ts(R("om", 0, 384), R("om", 0, 384), 15, None, OP.bitwise_and)
+    act(R("l32", 384, 512), M("BD"), AF.Identity, 0.0, -1.0)
+    asel(LZ, R("l32", 384, 512), [[0, 8], [1, 16]], OP.is_ge, 0.0, -8, 0, late)
+    ms(R("tab", W, W + 8), float(W))
     for t in range(RO):
-        ts(M("TR%d" % t), R("om", 128 * t, 128 * t + 128), col(t), BIG, OP.is_gt, OP.mult)
-    tr3 = R("mb", M("TR0")[1], M("TR2")[2])
-    asel(tr3, tr3, [[0, 3], [-16, 8], [0, 16]], OP.is_ge, 0.0, 0, 1)
-    asel(tr3, tr3, [[0, 3], [16, 8], [0, 16]], OP.is_ge, 0.0, 15, -1)
-    asel(tr3, tr3, [[0, 3], [-1, 128]], OP.not_equal, -BIG, 0, 1)
+        om, tr = R("om", 128 * t, 128 * t + 128), M("TR%d" % t)
+        iota(om, [[0, 8], [1, 16]], 32 - 5 * t, 0, late)
+        ts(om, om, 15, None, OP.bitwise_and)
+        ts(tr, om, col(t), BIG, OP.is_gt, OP.mult)
+        asel(tr, tr, [[-16, 8], [0, 16]], OP.is_ge, 0.0, 0, 1)
+        asel(tr, tr, [[16, 8], [0, 16]], OP.is_ge, 0.0, 15, -1)
+        asel(tr, tr, [[-1, 128]], OP.not_equal, -BIG, 0, 1)
+        soon[0] = None
+    ms(R("mhalf", 0, 128), -0.5)
+    ms(R("zb", 0, 144), 0.0)
+    ms(R("xt", W, W + 16), 0.0)
+    ts(R("zf", 144, 288), R("ones", 0, 144), 0.0, None, OP.mult)
+    ts(R("zf", 288, 432), R("ones", 0, 144), 0.0, None, OP.mult)
+    ts(R("c16", 0, 64), R("ones", 0, 64), -3000.0, None, OP.mult)
+    ts(col(21), col(22), 1 - KZ, -SH - 1, OP.mult, OP.add)
+    ts(R("zb", 15, 143, 16), bd8, R("cm", 0, 1), BIG, OP.mult, OP.mult)
+    ts(R("zf", 159, 287, 16), bd8, R("cm", 5, 6), None, OP.mult)
+    ts(R("zf", 303, 431, 16), bd8, R("cm", 8, 9), None, OP.mult)
+    for o in (0, 8):
+        act(R("b16", o, o + 8), bd8, AF.Identity)
+        act(R("b16", o + 16, o + 24), bd8, AF.Identity, 0.0, 0.5)
     ts(col(19), col(0), 2.0, None, OP.mult)
     ts(R("dw", 0, 16), R("dw", 0, 16), col(19), None, OP.add)
-    ms(R("tab", W, TW), float(W))
-    ms(R("xt", W, W + 16), 0.0)
-    soon[0] = None
     ts(R("w16", 512, 1024), R("w16", 0, 512), 1.0, None, OP.add)
     iota(R("io2", 0, 512), [[-32, 4], [0, 4], [-1, 32]], 0, 1, late)
     ts(R("rep", 0, 512), R("io2", 0, 512), 0.0, None, OP.is_equal)
@@ -330,7 +341,7 @@ def build(g, core, T, topo):
     soon[0] = None
 
     TAB, XT = R("tab", 0, W + 8), R("xt", 0, W + 16)
-    flip, eqs, last, clock = [0, 0, 0], [], [], [0.0]
+    flip, eqs, last, clock = [0, 0, 0, 0], [], [], [0.0]
 
     def chain(i):
         for j in last:
@@ -381,7 +392,8 @@ def build(g, core, T, topo):
                        False, (eb, a, b, s, kp) == tests[-1])
             if v1 != u1:
                 continue
-            t1, t2, t3 = R("p6", 0, n), R("p6", n, 2 * n), R("p6", 2 * n, 3 * n)
+            t1, t2 = R("p6", 0, n), R("p6", n, 2 * n)
+            wu = R("w16", 512 * par + u0, 512 * par + u1)
             tr = M("TR%d" % t)
             s1, s2 = R("sg", 256 * pc, 256 * pc + 128, 1, n), R("sg", 256 * pc + 128, 256 * pc + 256, 1, n)
             a1, ok = R("ao", 2 * u0, 2 * u0 + n), R("ao", 2 * u0 + n, 2 * u1)
@@ -389,12 +401,13 @@ def build(g, core, T, topo):
             b1, b2 = R(hb, 256, 256 + n), R(hb, 256 + n, 256 + 2 * n)
             mm([(b1, s1, M("I3", n)), (b2, s1, M("I", n)), (b2, s2, M("I", n))])
             act(R("ao", 2 * u0, 2 * u1), R(hb, 256, 256 + 2 * n), AF.Sign, -1.5)
-            mm([(t1, IF, U("s16")), (t2, SHF, U("s16")), (t3, IF, R("w16", 512 * par + u0, 512 * par + u1))], True, False)
-            mm([(t2, M("IB"), a1), (t3, M("NIB"), a1), (t1, tr, ok), (t2, tr, ok), (t3, tr, ok)], False, True)
-            rr = lambda a, b: R("rr", 3 * u0 + a * n, 3 * u0 + b * n)
-            act(rr(0, 3), R("p6", 0, 3 * n), AF.Relu, col(4 + t))
+            mm([(t1, IF, U("s16")), (t2, SHF, U("s16")), (t2, IF, wu)], True, False)
+            mm([(t2, M("IB"), a1), (t1, tr, ok), (t2, tr, ok)], False, True)
+            rr = lambda a, b: R("rr", 2 * u0 + a * n, 2 * u0 + b * n)
+            act(rr(0, 2), R("p6", 0, 2 * n), AF.Relu, col(4 + t))
             bz = R("p7", 0, n)
-            mm([(bz, LB, rr(0, 1)), (bz, LZ, rr(1, 2)), (bz, LZ, rr(2, 3))])
+            mm([(bz, IZ, wu)], True, False)
+            mm([(bz, LB, rr(0, 1)), (bz, LZ, rr(1, 2))], False, True)
             due(act(U("ab"), bz, AF.Abs, col(10)), RL * t + DUE["sel"][pc])
             for u0, u1 in [p for p in parts(VCH) if p[1] == u1]:
                 ts(U("ind"), U("ab"), 512.0, None, OP.is_lt)
@@ -419,12 +432,17 @@ def build(g, core, T, topo):
         mm([(R("p7", 4, 16), Z("zf", 1, a), R("c16", 128 + a, 320, 16)) for a in range(16)])
         ts(R("obz", 4, 16), R("p7", 4, 16), SH, None, OP.add)
         cp(R("eo", 64, 256), ("ind", TAB, R("obz", 4, 16)))
-        cp(R("xbz", 64, 256), ("ind", XT, R("obz", 4, 16)))
-        cp(R("xbz", 320, 512), ("ind", XT, R("obz", 20, 32)))
+        for o in (0, 256):
+            for lo, hi in ((o + 64, o + 128), (o + 128, o + 256)):
+                if lo - o < XV:
+                    cp(R("xbz", lo, hi), ("ind", XT, R("obz", lo // 16, hi // 16)))
+                else:
+                    due(act(R("xbz", lo, hi), ("ind", XT, R("obz", lo // 16, hi // 16)), AF.Identity), RL * t + DUE["xbz"])
         ts(R("sbf", 0, 256), R("eo", 0, 256), -SH, None, OP.add)
         ts(R("nj", 0, 256), R("eo", 0, 256), float(W), None, OP.is_equal)
-        mm([(R("p3", 0, 256), M("I"), R("xbz", 256, 512)), (R("p3", 0, 256), M("NI"), R("xbz", 0, 256))])
-        act(R("dzb", 0, 256), R("p3", 0, 256), AF.Abs)
+        for lo in (0, 128):
+            mm([(R("p6", lo, lo + 128), M("I"), R("xbz", 256 + lo, 384 + lo)), (R("p6", lo, lo + 128), M("NI"), R("xbz", lo, lo + 128))])
+            act(R("dzb", lo, lo + 128), R("p6", lo, lo + 128), AF.Abs)
         for a in range(16):
             dma("s", T.shf[a:128:16, 0:304], T.c16[5:128:16, 15 - a:319 - a], [R("c16", 15 - a, 319 - a)], [], "sf", 2500, eqs)
         landed(R("shf", 0, 304), "sf")
@@ -433,7 +451,7 @@ def build(g, core, T, topo):
         mm([(R("p1", 0, 256), M("BD"), R("eq", 256 * q, 256 * q + 256)) for q in range(4)])
         act(R("cnt", 0, 256), R("p1", 0, 256), AF.Identity)
         ts(R("bl", 0, 16), R("obz", 0, 16), -SH, None, OP.add)
-        mm([(R("p1", 0, 16), IF, R("bl", 0, 16))] + [(R("p1", 0, 16), Z("zb", 2, a), R("cnt", a, 256, 16)) for a in range(16)])
+        mm([(R("p1", 0, 16), IF, R("bl", 0, 16))] + [(R("p1", 0, 16), Z("zb", 0, a), R("cnt", a, 256, 16)) for a in range(16)])
         tt(R("tg", 0, 16), R("dw", 0, 16), R("p1", 0, 16), OP.min)
         if t < RO - 1:
             mm([(R("p1", 256 + 16 * s, 272 + 16 * s), blk("rep", s, 128), R("tg", 0, 16)) for s in range(N)])
@@ -442,45 +460,47 @@ def build(g, core, T, topo):
             s_o = send([(R("tg", 0, 16), blk("lt", rank, 16), peers)], "lt%d" % rank, off_eng)[0]
         due(len(ops) - 1, RL * t + DUE["mo"])
         sent = {}
+        flip[2] = 0
         clock[0] = RL * t + DUE["max"]
         for c0, c1 in parts(SUB):
-            st = (c1 - c0) // 32
-            dup = 16 // st
-            h, (s0, s1) = [(i, p) for i, p in enumerate(parts(JC[t])) if p[1] >= c1][0]
+            due(act(R("xe", 16 * c0, 16 * c1), ("ind", XT, R("eo", c0, c1)), AF.Identity), RL * t + DUE["xe"])
+        for h, (s0, s1) in enumerate(parts(JC[t])):
             n = s1 - s0
             H = lambda b, o=0: R(b, o + s0, o + s1)
             K = lambda b, k: R(b, 16 * s0 + k, 16 * s1, 16)
             hb = "p%d" % (4 + h % 2)
             r2, r1 = R(hb, 0, 128, 1, n), R(hb, 128, 256, 1, n)
-            act(R("xe", 16 * c0, 16 * c1), ("ind", XT, R("eo", c0, c1)), AF.Identity)
-            mm([(R("p2", d, 512, dup), M("I"), R("xbz", c0, c1)) for d in range(dup)])
             byv = [kp for kp in range(2) if (h, kp) not in ABS[t]]
-            if byv:
-                mm([(R("p0", d, 512, dup), M("I"), R("xbz", 256 + c0, 256 + c1)) for d in range(dup)])
-            if c1 == s1:
-                odd = lambda r, kp: R(r[0], r[1] + kp, r[2], 2, r[4])
-                mm([(r2, H("nj"), M("IB")), (r1, H("nj"), M("IB")), (r2, H("xbz"), M("BDH")), (r1, H("dzb"), M("NBDH"))] +
-                   [(odd(r, kp), H("xbz", 256), odd(M("NBDH"), kp)) for kp in byv for r in (r1, r2)], True, False)
-                for kp in range(2):
-                    o, w8 = (128, g8("NBDH")) if kp in byv else (0, g8("BDH"))
-                    mm([(R(hb, o + k, o + 128, 16, n), K("xe", k), w8) for k in range(kp, 16, 2)], False, False)
-            items = [(kp, eb) for kp in range(st) for eb in ("e2", "e1")]
-            items = [x for x in items if x[1] == "e2" or x[0] in byv] + [x for x in items if x[1] == "e1" and x[0] not in byv]
-            for kp, eb in items:
-                xs = R("xe", 16 * c0 + kp, 16 * c1, st)
-                tgt, hi, w8 = ("p2", 128, g8("NBD")) if eb == "e2" else ("p0", 256, R("b16", 0, 16))
-                if eb == "e1" and kp not in byv:
-                    bank = "p%d" % (3 + 4 * (flip[2] % 2))
-                    flip[2] += 1
-                    mm([(R(bank, 0, 512), M("I"), xs)] + [(R(bank, d, 512, dup), M("NI"), R("xbz", 256 + c0, 256 + c1)) for d in range(dup)])
-                    due(act(R(eb, xs[1], xs[2], st), R(bank, 0, 512), AF.Abs), clock[0] + DUE["abs"])
-                    w8 = R("b16", 16, 32)
-                else:
-                    chain(tt(R(eb, xs[1], xs[2], st), xs, R(tgt, 0, 512), OP.max))
+            odd = lambda r, kp: R(r[0], r[1] + kp, r[2], 2, r[4])
+            for c0, c1 in [(s0 + a, s0 + b) for a, b in (parts([64] * (n // 64)) if h == 0 else [(0, n)])]:
+                st = (c1 - c0) // 32
+                bb, bz = SPREAD[flip[2] % 2]
+                flip[2] += 1
+                mm([(R(bb, d, 512, 16 // st), M("I"), R("xbz", c0, c1)) for d in range(16 // st)])
+                if byv:
+                    mm([(R(bz, d, 512, 16 // st), M("I"), R("xbz", 256 + c0, 256 + c1)) for d in range(16 // st)])
                 if c1 == s1:
-                    mm([(R(hb, k, hi, 16, n), K(eb, k), w8) for k in range(kp, 16, st)], False, (kp, eb) == items[-1])
-            if c1 != s1:
-                continue
+                    mm([(r2, H("nj"), M("IB")), (r1, H("nj"), M("IB")), (r2, H("xbz"), M("BDH")), (r1, H("dzb"), M("NBDH"))] +
+                       [(odd(r, kp), H("xbz", 256), odd(M("NBDH"), kp)) for kp in byv for r in (r1, r2)], True, False)
+                    for kp in range(2):
+                        o, w8 = (128, g8("NBDH")) if kp in byv else (0, g8("BDH"))
+                        mm([(R(hb, o + k, o + 128, 16, n), K("xe", k), w8) for k in range(kp, 16, 2)], False, False)
+                items = [(kp, eb) for kp in range(st) for eb in ("e2", "e1")]
+                items = [x for x in items if x[1] == "e2" or x[0] % 2 in byv] + [x for x in items if x[1] == "e1" and x[0] % 2 not in byv]
+                for kp, eb in items:
+                    xs = R("xe", 16 * c0 + kp, 16 * c1, st)
+                    tgt, hi, w8 = (bb, 128, g8("NBD")) if eb == "e2" else (bz, 256, R("b16", 0, 16))
+                    if eb == "e1" and kp % 2 not in byv:
+                        bank = SPREAD[flip[2] % 2][flip[3] % 2]
+                        flip[3] += 1
+                        mm([(R(bank, 0, 512), M("I"), xs)] +
+                           [(R(bank, d, 512, 16 // st), M("NI"), R("xbz", 256 + c0, 256 + c1)) for d in range(16 // st)])
+                        due(act(R(eb, xs[1], xs[2], st), R(bank, 0, 512), AF.Abs), clock[0] + DUE["abs"])
+                        w8 = R("b16", 16, 32)
+                    else:
+                        chain(tt(R(eb, xs[1], xs[2], st), xs, R(tgt, 0, 512), OP.max))
+                    if c1 == s1:
+                        mm([(R(hb, k, hi, 16, n), K(eb, k), w8) for k in range(kp, 16, st)], False, (kp, eb) == items[-1])
             pu, px = R("p6", 0, n), R("p6", 128, 128 + n)
             mm([(pu, M("I4"), R("mhalf", 0, n)), (px, SEL(8), H("c16", 64)), (px, M("IB"), R("ones", 0, n)), (px, M("TR0"), H("nj"))], True, False)
             ev, rf = R("er", 2 * s0, 2 * s0 + n), R("er", 2 * s0 + n, 2 * s1)
@@ -492,9 +512,9 @@ def build(g, core, T, topo):
             due(tt(H("md"), H("uu"), px, OP.min), RL * t + DUE["md"][h if s1 < 256 else 2])
             if t < RO - 1:
                 got = lambda s, k=1: R("mf32", 4 * s0 + n * s, 4 * s0 + n * (s + k))
-                mm([(R("p1", n * s, n * s + n), blk("rep", s, 128), H("md")) for s in range(N)])
-                act(got(2, 2), R("p1", 2 * n, 4 * n), AF.Identity, SH)
-                act(got(0, 2), R("p1", 0, 2 * n), AF.Identity, SH)
+                for bank, lo, hi in (("p1", 3, 4), ("p6", 2, 3), ("p1", 0, 2)) if s1 == 256 else (("p1", 0, 4),):
+                    mm([(R(bank, n * s, n * s + n), blk("rep", s, 128), H("md")) for s in range(lo, hi)])
+                    act(got(lo, hi - lo), R(bank, lo * n, hi * n), AF.Identity, SH)
                 for s in range(N - 1, -1, -1):
                     due(scat(R("tab", 0, TW), R("mo", 16 * s + s0 // 16, 16 * s + s1 // 16), got(s)), RL * t + DUE["tab"][h])
             else:
@@ -537,15 +557,8 @@ def build(g, core, T, topo):
     return ops, Q, nloc[0]
 
 
-def plan(ops):
+def order(ops, kids, key):
     n = len(ops)
-    kids = [[] for _ in range(n)]
-    for i, o in enumerate(ops):
-        for j in o["deps"]:
-            kids[j].append(i)
-    key = [0.0] * n
-    for i in range(n - 1, -1, -1):
-        key[i] = min([ops[i]["due"]] + [key[k] - HOP - ops[i]["cost"] - max(ops[i]["lat"], 0.0) for k in kids[i]])
     left = [len(o["deps"]) for o in ops]
     rdy = [0.0] * n
     pool = {e: [] for e in "vapgsx"}
@@ -555,7 +568,7 @@ def plan(ops):
             pool[ops[i]["eng"]].append(i)
     seq = []
     while len(seq) < n:
-        t0, e = min((max(free[e], min(rdy[i] for i in pool[e])), e) for e in pool if pool[e])
+        t0, e = min((max(free[e], min([rdy[i] for i in p])), e) for e, p in pool.items() if p)
         i = min([i for i in pool[e] if rdy[i] <= t0 + LOOK], key=lambda i: key[i])
         pool[e].remove(i)
         t0 = max(t0, rdy[i])
@@ -569,6 +582,49 @@ def plan(ops):
             if left[k] == 0:
                 pool[ops[k]["eng"]].append(k)
     return seq
+
+
+def span(ops, seq, pe, ga, hop):
+    done = [0.0] * len(ops)
+    free = {e: 0.0 for e in "vapgsx"}
+    for i in seq:
+        o = ops[i]
+        t0 = max([free[o["eng"]]] + [done[j] + (hop if h else 0.0) for j, h in o["deps"].items()])
+        c = o["cost"] * (pe if o["pe"] else 1.0) + CYC * (ga - GA) * o["ga"]
+        if o["eng"] != "x":
+            free[o["eng"]] = t0 + c
+        done[i] = t0 + c + max(o["lat"], 0.0)
+    return max(done)
+
+
+FOUND = {}
+
+
+def plan(ops):
+    n = len(ops)
+    kids = [[] for _ in range(n)]
+    for i, o in enumerate(ops):
+        for j in o["deps"]:
+            kids[j].append(i)
+    key = [0.0] * n
+    for i in range(n - 1, -1, -1):
+        key[i] = min([ops[i]["due"]] + [key[k] - HOP - ops[i]["cost"] - max(ops[i]["lat"], 0.0) for k in kids[i]])
+    shifted = lambda shift: order(ops, kids, [k + shift.get(o["tag"], 0.0) for k, o in zip(key, ops)])
+    if "shift" not in FOUND:
+        score = lambda q: sum(span(ops, q, *f) for f in FIGS)
+        rng = np.random.default_rng(1)
+        tags = sorted(set(o["tag"] for o in ops if o["tag"] < 1000))
+        shift = {}
+        best = score(shifted(shift))
+        for _ in range(TRIES):
+            cand = dict(shift)
+            for k in rng.choice(len(tags), int(rng.integers(1, 5))):
+                cand[tags[int(k)]] = float(rng.normal()) * float(rng.choice([500.0, 2000.0, 8000.0]))
+            val = score(shifted(cand))
+            if val <= best:
+                best, shift = val, cand
+        FOUND["shift"] = shift
+    return shifted(FOUND["shift"])
 
 
 def emit(g, T, ops, Q, nloc):

import numpy as np
from concourse.bass import DstId, RemoteDMATransfer
from concourse.mybir import AluOpType as OP, ActivationFunctionType as AF

N, V, W, RO = 4, 1024, 4096, 3
SH = 2048.0
BIG = 8192.0
KZ = (1 - SH + BIG) / 2
TW = W + 8 + 512
C0 = 520
CH = [32, 32] + [64] * 7
PCH = [128, 128, 128, 128]
VCH = [384, 128]
SUB = [64, 64, 64, 64]
JC = [[128, 128], [128, 128], [128, 64, 64]]
ABS = [[(1, 1)], [(1, 1)], [(2, 1)]]
XV = 128
SPREAD = [("p2", "p0"), ("p7", "p3")]
CYC, PEC, GA, SC, HOP, LOOK = 0.83, 0.42, 1.56, 3.8, 100.0, 100.0
FIGS = ((1.0, 1.56, 100.0), (0.85, 1.15, 160.0), (1.15, 2.0, 60.0))
RL, TRIES = 60000.0, 1400
DUE = {"test": 1500, "sel": [-1700, 11600, 11900, 17500], "pack": [30300, 31700], "mo": 30700, "max": 29400, "abs": -5900,
       "md": [26400, 31500, 44100], "tab": [41800, 39100], "xbz": 24000, "xe": 27000, "const": -2300, "load": -19500}
MATS = ["I", "NI", "IB", "ISH", "BDH", "NBDH", "BDB", "NBDB", "I4", "TR0", "TR1", "TR2", "BD", "S1", "S2", "NBD", "I3"]
F, B, H16, U16, I32 = "float32", "bfloat16", "float16", "uint16", "int32"
SCRATCH = {n: ("sbuf", [128, w], d) for n, w, d in [
    ("sti", V, I32), ("out", V, H16), ("lan", V, H16), ("xs", V, B), ("xl", V, B), ("io1", 512, B), ("io2", 512, B), ("un", 512, H16),
    ("rep", 512, H16), ("pq", 896, H16), ("cm", 16, F), ("ai", 64, I32), ("ao2", 64, U16), ("stg", V, F), ("ls", V, F), ("mf32", 1024, F),
    ("lm", 256, H16), ("lt", 64, H16), ("tab", TW, F), ("xt", W + 16, B), ("gg", 8192, F), ("e1", 8192, B), ("e2", 8192, B),
    ("xe", 4096, B), ("mb", 128 * len(MATS), B), ("sel", 2048, H16), ("mf", 384, H16), ("l32", 512, F), ("zb", 144, B),
    ("zf", 432, H16), ("ones", 256, B), ("mhalf", 128, B), ("cc", 24, F), ("ci", 8, I32), ("om", 384, I32), ("wf", 512, F),
    ("w16", 1024, H16), ("dw", 16, F), ("s16", 512, H16), ("so", 512, U16), ("non", 512, B), ("sg", 1536, B), ("ao", 1024, B),
    ("b16", 32, B), ("rr", 1024, F), ("ab", 512, F), ("ind", 512, H16), ("val", 512, H16), ("prod", 512, H16),
    ("co", 32, U16), ("cb", 2576, F), ("c16", 320, H16), ("obz", 32, U16), ("eo", 256, U16), ("xbz", 512, B), ("sbf", 256, H16),
    ("nj", 256, B), ("dzb", 256, B), ("fl", 768, B), ("er", 512, B), ("uu", 256, H16), ("shf", 304, H16), ("bl", 16, H16),
    ("eq", 1024, B), ("cnt", 256, B), ("tg", 16, H16), ("md", 256, H16), ("mo", 64, U16), ("yb", TW, F)]}
for _i in range(8):
    SCRATCH["p%d" % _i] = ("psum", [128, 512], F)
SEMAPHORES = ["qv", "qa", "qp", "qg", "ldx", "xt", "yb", "sf", "st0", "st1", "loc"]
for _s in range(N):
    SEMAPHORES += [_n + str(_s) for _n in ("ld", "sa", "sx", "sy", "sg", "lm", "lt")]


def transfer(topo, dst_cores, src, dst, sem, engines):
    ids = [DstId(rid=topo.addr(d)[0], pnc=topo.addr(d)[1]) for d in dst_cores]
    return RemoteDMATransfer(dst_ids=ids, dma_engine_mask=sum(1 << e for e in engines), remote_sem=sem, srcs=[src], dsts=[dst] * len(ids))


def common_engines(src, dsts, topo):
    return [e for e in topo.engines(src, dsts[0]) if all(e in topo.engines(src, d) for d in dsts)]


def R(name, lo, hi, st=1, rows=128):
    return (name, lo, hi, st, rows)


def width(r):
    return len(range(r[1], r[2], r[3]))


def bits(r):
    return (((1 << (width(r) * r[3])) - 1) // ((1 << r[3]) - 1)) << r[1]


def parts(sizes):
    ends = [sum(sizes[:i + 1]) for i in range(len(sizes))]
    return [(e - n, e) for e, n in zip(ends, sizes)]


def build(g, core, T, topo):
    rank = T.rank_of(core)
    peers = [c for c in T.cores if c != core]
    off_eng = common_engines(core, peers, topo)
    NE = len(off_eng)
    ops, acc, nloc, base, ndma, soon = [], {}, [0], [-1000], {}, [None]
    Q = {"v": g.vector, "a": g.scalar, "p": g.tensor, "g": g, "s": g.sync}

    def ap(r):
        return T[r[0]][0:r[4], r[1]:r[2]:r[3]] if r[3] != 1 else T[r[0]][0:r[4], r[1]:r[2]]

    def add(eng, fn, cost, rd=(), wr=(), after=(), sem=None, val=0, lat=0.0, ga=0):
        i = len(ops)
        deps = {}
        for r, w in [(r, False) for r in rd] + [(r, True) for r in wr]:
            ps = SCRATCH[r[0]][0] == "psum"
            m = bits(r)
            keep = []
            for (j, mj, wj) in acc.get(r[0], []):
                if j == i:
                    keep.append((j, mj, wj))
                    continue
                same = ops[j]["eng"] == eng and ops[j]["sem"] is None and sem is None
                hit = bool(m & mj) and (w or wj)
                if ps and (not same or eng == "p"):
                    hit = True
                if hit:
                    deps[j] = deps.get(j, False) or not (same and eng == "p")
                if not (w and (mj & ~m) == 0 and hit):
                    keep.append((j, mj, wj))
            keep.append((i, m, w))
            acc[r[0]] = keep
        for j in after:
            deps[j] = deps.get(j, False)
        ops.append({"eng": eng, "fn": fn, "cost": cost, "deps": deps, "sem": sem, "val": val, "lat": lat,
                    "tag": i - base[0], "ga": ga, "pe": eng == "p", "due": RL * RO if soon[0] is None else soon[0]})
        return i

    def sc(x):
        return ap(x) if isinstance(x, tuple) else x

    def src(x):
        if x[0] == "ind":
            return ap(x[1]).indirect(ap(x[2])), [x[1], x[2]], GA
        return ap(x), [x], 1.0

    def two(*rs):
        return all(SCRATCH[r[0]][2] in (B, H16, U16) for r in rs)

    def ts(out, in0, s1, s2, o0, o1=None):
        a, rd, f = src(in0)
        if f == 1.0 and two(out, in0):
            f = 0.5
        rd = rd + [s for s in (s1, s2) if isinstance(s, tuple)]
        if o1 is None:
            fn = lambda: g.vector.tensor_scalar(ap(out), a, sc(s1), None, o0)
        else:
            fn = lambda: g.vector.tensor_scalar(ap(out), a, sc(s1), sc(s2), o0, o1)
        return add("v", fn, 60 + CYC * max(64, f * width(out)), rd, [out], ga=width(out) if f == GA else 0)

    def tt(out, a, b, o):
        f = 1 if SCRATCH[b[0]][0] == "psum" else 2
        return add("v", lambda: g.vector.tensor_tensor(ap(out), ap(a), ap(b), o), 60 + CYC * max(64, f * width(out)), [a, b], [out])

    def cp(out, in_):
        a, rd, f = src(in_)
        if f == 1.0 and two(out, in_):
            f = 0.5
        return add("v", lambda: g.vector.tensor_copy(ap(out), a), 60 + CYC * max(64, f * width(out)), rd, [out], ga=width(out) if f == GA else 0)

    def scat(win, off, a):
        return add("v", lambda: g.vector.tensor_copy(ap(win).indirect(ap(off)), ap(a)), 60 + CYC * SC * width(a), [off, a], [win])

    def ms(out, c):
        return add("v", lambda: g.vector.memset(ap(out), c), 60 + CYC * max(64, width(out)), [], [out])

    def scan(out, d0, d1, init, o0, o1):
        rd = [d0, d1] + ([init] if isinstance(init, tuple) else [])
        f = 0.5 if two(out, d0, d1) else 1.0
        return add("v", lambda: g.vector.tensor_tensor_scan(ap(out), ap(d0), ap(d1), sc(init), o0, o1), 60 + CYC * max(64, f * width(out)), rd, [out])

    def act(out, in_, func, bias=0.0, scale=1.0):
        a, rd, f = src(in_)
        rd = rd + ([bias] if isinstance(bias, tuple) else [])
        return add("a", lambda: g.scalar.activation(ap(out), a, func, bias=sc(bias), scale=scale), 80 + CYC * max(64, f * width(out)), rd, [out],
                   ga=width(out) if f == GA else 0)

    def mm(terms, start=True, stop=True):
        def fn():
            for n, (o, l, r) in enumerate(terms):
                ins = g.tensor.matmul(ap(o), ap(l), ap(r), start and n == 0, stop and n == len(terms) - 1)
            return ins
        cost = 30 + sum(PEC * max(64, width(r)) * (4 if SCRATCH[r[0]][2] == F else 1) for (o, l, r) in terms)
        return add("p", fn, cost, list(set([l for (o, l, r) in terms] + [r for (o, l, r) in terms])), list(set(o for (o, l, r) in terms)))

    def iota(out, pat, start, cm, after=()):
        if SCRATCH[out[0]][2] == I32:
            fn = lambda: g.iota(ap(out), pat, start, cm)
        else:
            fn = lambda: g.iota(ap(out), pat, start, cm, allow_small_or_imprecise_dtypes=True)
        return add("g", fn, 150 + 2 * CYC * width(out), [], [out], after)

    def asel(out, a, pat, cmp, fill, start, cm, after=()):
        return add("g", lambda: g.affine_select(ap(out), ap(a), pat, cmp, fill, start, cm), 200 + 2 * CYC * width(out), [a], [out], after)

    def send(pieces, sem, engines, after=()):
        k = 1 << (len(engines) // len(pieces)).bit_length() - 1
        nloc[0] += k * len(pieces)
        fn = lambda: g.remote_dma_fused([transfer(topo, d, ap(r), ap(to), T.sem[sem], engines[k * n:k * n + k])
                                         for n, (r, to, d) in enumerate(pieces)], local_sem=T.sem.loc)
        return add("g", fn, 700, [r for r, to, d in pieces], [], after, lat=-1.0), k

    def dma(q, out, in_, rd, wr, sem, lat, after=()):
        ndma[sem] = ndma.get(sem, 0) + 16
        i = add(q, lambda: Q[q].dma_start(out, in_), 50, rd, wr, sem=sem, val=ndma[sem], lat=lat)
        for j in after:
            ops[i]["deps"][j] = True
        return i

    def arrive(r, sem, val, after, lat):
        return add("x", None, 0, [], [r], after, sem=sem, val=val, lat=lat)

    def landed(r, sem):
        return add("x", None, 0, [], [r], [i for i, o in enumerate(ops) if o["sem"] == sem], sem=sem, val=ndma[sem])

    def due(i, at):
        ops[i]["due"] = at
        return i

    def M(name, n=128):
        k = MATS.index(name)
        return R("mb", 128 * k, 128 * k + n, 1, n)

    def g8(name):
        return R("mb", M(name)[1], M(name)[2], 16)

    def Z(buf, n, k):
        return R(buf, 144 * n + 15 - k, 144 * n + 143 - k)

    def SEL(k):
        return R("sel", 128 * k, 128 * k + 128)

    def PQ(s, q):
        return R("pq", 224 * q + 96 - 32 * s, 224 * q + 224 - 32 * s)

    def col(k):
        return R("cc", k, k + 1)

    IF, SHF, IZ = R("mf", 0, 128), R("mf", 128, 256), R("mf", 256, 384)
    LB, LZ = R("l32", 0, 128), R("l32", 128, 256)
    ring = [(rank + 1 + j) % N for j in range(N)]
    blk = lambda b, d, n=256: R(b, n * d, n * d + n)
    rows = lambda d: slice(32 * d, 32 * d + 32)
    soon[0] = DUE["load"]
    lds = [dma("sa"[n % 2], ap(blk("sti", d)), T.stars[rows(d), :], [], [blk("sti", d)], "ld%d" % d, 2400 + 100 * n) for n, d in enumerate(ring)]
    s_a = []
    for d in ring[:-1]:
        ts(blk("out", d), blk("sti", d), -SH, None, OP.add)
        s_a.append(send([(blk("out", d), blk("lan", rank), [T.cores[d]])], "sa%d" % rank, off_eng, s_a[-1:])[0])
    ts(blk("lan", rank), blk("sti", rank), -SH, None, OP.add)
    soon[0] = DUE["const"]
    for d in ring[:-1]:
        dma("s", ap(blk("xs", d)), T.x[rows(d), :], [], [blk("xs", d)], "ldx", 2500, lds)
    landed(R("xs", 0, V), "ldx")
    s_x, kx = send([(blk("xs", d), blk("xl", rank), [T.cores[d]]) for d in ring[:-1]], "sx%d" % rank, off_eng, s_a[-1:])
    for s in ring[::-1]:
        if s != rank:
            arrive(blk("xl", s), "sx%d" % s, kx, [s_x], 6000)
        for q in range(N):
            if s == rank:
                dma("s", T.xt[rows(q), V * s:V * s + V], T.x[rows(s), :], [], [], "xt", 2500, lds)
            else:
                dma("s", T.xt[rows(q), V * s:V * s + V], ap(blk("xl", s)), [blk("xl", s)], [], "xt", 3000)
    landed(R("xt", 0, W), "xt")

    ms(R("ones", 0, 256), 1.0)
    ts(R("zf", 0, 144), R("ones", 0, 144), 0.0, None, OP.mult)
    iota(R("ci", 0, 8), [[0, 2], [-5, 4]], 32, 1)
    iota(R("io1", 0, 512), [[-1, 4], [0, 4], [-4, 32]], 0, 1)
    ts(R("un", 0, 512), R("io1", 0, 512), 0.0, None, OP.is_equal)
    asel(M("BD"), R("ones", 0, 128), [[-16, 8], [0, 16]], OP.is_ge, 0.0, 0, 1)
    asel(M("BD"), M("BD"), [[16, 8], [0, 16]], OP.is_ge, 0.0, 15, -1)
    asel(M("I"), R("ones", 0, 128), [[-1, 128]], OP.is_equal, 0.0, 0, 1)
    late = s_a[-1:]
    asel(M("S1"), M("BD"), [[-1, 128]], OP.is_equal, 0.0, -1, 1, late)
    asel(M("S2"), M("BD"), [[-1, 128]], OP.is_equal, 0.0, 15, 1, late)
    iota(R("wf", 0, 512), [[2, 512]], -int(SH), 0, late)
    iota(R("ai", 0, 64), [[1, 2], [32, 32]], 0, 0, late)
    iota(R("dw", 0, 16), [[32, 16]], W + 8 - int(SH), 0, late)
    iota(R("cm", 0, 16), [[1, 16]], 0, 0)
    ts(R("ci", 5, 6), R("ci", 4, 5), rank + 1, None, OP.add)
    ts(R("ci", 5, 6), R("ci", 5, 6), 3, None, OP.bitwise_and)
    ts(R("ci", 4, 5), R("ci", 4, 5), 5, None, OP.arith_shift_right)
    cp(R("cc", 16, 18), R("ci", 4, 6))
    ts(R("ci", 0, 4), R("ci", 0, 4), 15, None, OP.bitwise_and)
    cp(R("cc", 0, 4), R("ci", 0, 4))
    ts(R("cc", 4, 7), R("cc", 0, 3), -BIG, SH + 1 - BIG, OP.mult, OP.add)
    ts(col(14), col(0), 4.0, None, OP.is_lt)
    ts(col(7), col(14), col(0), 512.0, OP.mult, OP.mult)
    ts(col(8), col(0), 4.0, None, OP.is_equal)
    ts(col(9), col(14), col(8), None, OP.subtract)
    ts(col(10), col(17), -1024.0, -512.5, OP.mult, OP.add)
    ts(col(10), col(10), col(14), None, OP.mult)
    ts(col(22), col(0), 8.0, None, OP.is_ge)
    ts(col(10), col(22), SH + KZ, col(10), OP.mult, OP.add)
    ts(IZ, M("I"), col(22), None, OP.mult)
    ts(col(10), col(8), 511.5, col(10), OP.mult, OP.add)
    ts(col(16), col(16), 1024.0, -1024.0, OP.mult, OP.add)
    ts(R("w16", 0, 512), R("wf", 0, 512), col(16), None, OP.add)
    ts(col(18), col(0), 2.0, col(16), OP.mult, OP.add)
    ts(R("ao2", 0, 64), R("ai", 0, 64), col(18), None, OP.add)
    ts(R("cm", 0, 16), R("cm", 0, 16), col(0), None, OP.is_equal)
    bd8 = g8("BD")
    ts(R("zf", 15, 143, 16), bd8, col(9), None, OP.mult)
    for k in range(16):
        ts(SEL(k), M("BD"), R("cm", k, k + 1), None, OP.mult)
    for nm, of, f in (("NI", "I", -1.0), ("IB", "I", BIG), ("I4", "I", 4096.0), ("I3", "I", 3.0), ("BDH", "BD", 0.5),
                      ("NBDH", "BD", -0.5), ("BDB", "BD", BIG), ("NBDB", "BD", -BIG), ("NBD", "BD", -1.0)):
        act(M(nm), M(of), AF.Identity, 0.0, f)
    mm([(R("p0", 0, 128), M("I"), M("S1")), (R("p0", 0, 128), M("I"), M("S2"))] + [(R("p0", 128, 256), M("I"), M(x)) for x in ("S1", "S2", "I")])
    act(M("ISH"), R("p0", 128, 256), AF.Identity)
    cp(SHF, R("p0", 0, 128))
    cp(IF, M("I"))
    act(R("l32", 256, 384), M("BD"), AF.Identity)
    asel(LB, R("l32", 256, 384), [[0, 8], [-1, 16]], OP.is_ge, 0.0, 7, 0, late)
    act(R("l32", 384, 512), M("BD"), AF.Identity, 0.0, -1.0)
    asel(LZ, R("l32", 384, 512), [[0, 8], [1, 16]], OP.is_ge, 0.0, -8, 0, late)
    ms(R("tab", W, W + 8), float(W))
    for t in range(RO):
        om, tr = R("om", 128 * t, 128 * t + 128), M("TR%d" % t)
        iota(om, [[0, 8], [1, 16]], 32 - 5 * t, 0, late)
        ts(om, om, 15, None, OP.bitwise_and)
        ts(tr, om, col(t), BIG, OP.is_gt, OP.mult)
        asel(tr, tr, [[-16, 8], [0, 16]], OP.is_ge, 0.0, 0, 1)
        asel(tr, tr, [[16, 8], [0, 16]], OP.is_ge, 0.0, 15, -1)
        asel(tr, tr, [[-1, 128]], OP.not_equal, -BIG, 0, 1)
        soon[0] = None
    ms(R("mhalf", 0, 128), -0.5)
    ms(R("zb", 0, 144), 0.0)
    ms(R("xt", W, W + 16), 0.0)
    ts(R("zf", 144, 288), R("ones", 0, 144), 0.0, None, OP.mult)
    ts(R("zf", 288, 432), R("ones", 0, 144), 0.0, None, OP.mult)
    ts(R("c16", 0, 64), R("ones", 0, 64), -3000.0, None, OP.mult)
    ts(col(21), col(22), 1 - KZ, -SH - 1, OP.mult, OP.add)
    ts(R("zb", 15, 143, 16), bd8, R("cm", 0, 1), BIG, OP.mult, OP.mult)
    ts(R("zf", 159, 287, 16), bd8, R("cm", 5, 6), None, OP.mult)
    ts(R("zf", 303, 431, 16), bd8, R("cm", 8, 9), None, OP.mult)
    for o in (0, 8):
        act(R("b16", o, o + 8), bd8, AF.Identity)
        act(R("b16", o + 16, o + 24), bd8, AF.Identity, 0.0, 0.5)
    ts(col(19), col(0), 2.0, None, OP.mult)
    ts(R("dw", 0, 16), R("dw", 0, 16), col(19), None, OP.add)
    ts(R("w16", 512, 1024), R("w16", 0, 512), 1.0, None, OP.add)
    iota(R("io2", 0, 512), [[-32, 4], [0, 4], [-1, 32]], 0, 1, late)
    ts(R("rep", 0, 512), R("io2", 0, 512), 0.0, None, OP.is_equal)
    for q in range(N):
        ts(R("pq", 224 * q, 224 * q + 224), R("ones", 0, 224), 0.0, None, OP.mult)
        cp(R("pq", 224 * q + 96, 224 * q + 128), R("rep", 128 * q, 128 * q + 32))

    soon[0] = DUE["load"]
    for n, s in enumerate([rank] + ring[-2::-1]):
        if s != rank:
            arrive(blk("lan", s), "sa%d" % s, NE, [s_a[n - 1]], 3500)
        for h in range(2):
            bank = "p%d" % (2 * (n % 2) + h + 4)
            mm([(R(bank, 256 * c, 256 * c + 256), blk("un", 2 * h + c, 128), blk("lan", s)) for c in range(2)])
            to = R("tab", V * s + 512 * h, V * s + 512 * h + 512)
            if h == 0:
                act(to, R(bank, 0, 512), AF.Identity, SH)
            else:
                ts(to, R(bank, 0, 512), SH, None, OP.add)
    soon[0] = None

    TAB, XT = R("tab", 0, W + 8), R("xt", 0, W + 16)
    flip, eqs, last, clock = [0, 0, 0, 0], [], [], [0.0]

    def chain(i):
        for j in last:
            ops[i]["deps"].setdefault(j, False)
        last[:] = [due(i, clock[0])]
        clock[0] += ops[i]["cost"]

    for t in range(RO):
        par = t % 2
        base[0] = len(ops)
        own = lambda a, b: ("ind", TAB, R("ao2", 32 * par + a // 16, 32 * par + b // 16))
        cp(R("so", 0, 64), own(0, 64))
        ts(R("s16", 0, 64), R("so", 0, 64), -SH, None, OP.add)
        ts(R("s16", 64, 512), own(64, 512), -SH, None, OP.add)
        ts(R("so", 64, 512), R("s16", 64, 512), SH, None, OP.add)
        ts(R("non", 0, 512), R("s16", 0, 512), SH, None, OP.is_equal)
        for o in range(N):
            iota(R("cb", C0 + 1 + 512 * o, C0 + 65 + 512 * o), [[0, 64]], 30000, 0)
        clock[0] = RL * t + DUE["test"]
        for v0, v1 in parts(CH):
            st = (v1 - v0) // 32
            pc, (u0, u1) = [(i, p) for i, p in enumerate(parts(PCH)) if p[1] >= v1][0]
            n = u1 - u0
            U = lambda b: R(b, u0, u1)
            act(R("gg", 16 * v0, 16 * v1), ("ind", TAB, R("so", v0, v1)), AF.Identity, -SH)
            if v0 == u0:
                flip[1] += 1
                hb = "p%d" % (4 + flip[1] % 2)
                mm([(R(hb, 0, 128, 1, n), U("non"), M("I")), (R(hb, 128, 256, 1, n), U("non"), M("ISH"))], True, False)
            w0, w1 = (v0, v1) if pc == 0 else (u0, u1)
            sw = (w1 - w0) // 32
            tests = [("e2", v0, v1, st, kp) for kp in range(st)]
            if v1 == w1:
                ws = [("e1", w0, w1, sw, kp) for kp in range(sw)]
                tests = [x for p in zip(ws, tests) for x in p] + ws[st:]
            if v0 == w0:
                mm([(R("p2", d, 512, 16 // sw), IF, R("w16", 512 * par + w0, 512 * par + w1)) for d in range(16 // sw)])
            for eb, a, b, s, kp in tests:
                tgt, o = "p2", 0
                if eb == "e2":
                    tgt, o = "p%d" % (flip[0] % 2), 128
                    flip[0] += 1
                    mm([(R(tgt, d, 512, 16 // s), SEL((s * d + kp + 1) % 16), R("s16", a, b)) for d in range(16 // s)])
                gs = R("gg", 16 * a + kp, 16 * b, s)
                chain(tt(R(eb, gs[1], gs[2], s), gs, R(tgt, 0, 512), OP.is_equal))
                if b == u1:
                    mm([(R(hb, o + k, o + 128, 16, n), R(eb, 16 * u0 + k, 16 * u1, 16), bd8) for k in range(kp, 16, s)],
                       False, (eb, a, b, s, kp) == tests[-1])
            if v1 != u1:
                continue
            t1, t2 = R("p6", 0, n), R("p6", n, 2 * n)
            wu = R("w16", 512 * par + u0, 512 * par + u1)
            tr = M("TR%d" % t)
            s1, s2 = R("sg", 256 * pc, 256 * pc + 128, 1, n), R("sg", 256 * pc + 128, 256 * pc + 256, 1, n)
            a1, ok = R("ao", 2 * u0, 2 * u0 + n), R("ao", 2 * u0 + n, 2 * u1)
            act(R("sg", 256 * pc, 256 * pc + 256, 1, n), R(hb, 0, 256, 1, n), AF.Sign)
            b1, b2 = R(hb, 256, 256 + n), R(hb, 256 + n, 256 + 2 * n)
            mm([(b1, s1, M("I3", n)), (b2, s1, M("I", n)), (b2, s2, M("I", n))])
            act(R("ao", 2 * u0, 2 * u1), R(hb, 256, 256 + 2 * n), AF.Sign, -1.5)
            mm([(t1, IF, U("s16")), (t2, SHF, U("s16")), (t2, IF, wu)], True, False)
            mm([(t2, M("IB"), a1), (t1, tr, ok), (t2, tr, ok)], False, True)
            rr = lambda a, b: R("rr", 2 * u0 + a * n, 2 * u0 + b * n)
            act(rr(0, 2), R("p6", 0, 2 * n), AF.Relu, col(4 + t))
            bz = R("p7", 0, n)
            mm([(bz, IZ, wu)], True, False)
            mm([(bz, LB, rr(0, 1)), (bz, LZ, rr(1, 2))], False, True)
            due(act(U("ab"), bz, AF.Abs, col(10)), RL * t + DUE["sel"][pc])
            for u0, u1 in [p for p in parts(VCH) if p[1] == u1]:
                ts(U("ind"), U("ab"), 512.0, None, OP.is_lt)
                scan(U("val"), U("ind"), U("ind"), col(7) if u0 == 0 else col(20), OP.add, OP.max)
                scan(U("prod"), U("val"), U("ind"), 0.0, OP.max, OP.mult)
                if u1 < 512:
                    cp(col(20), R("val", u1 - 1, u1))
                ob = R("p3", 0, (u1 - u0) // 16)
                mm([(ob, Z("zf", 0, a), R("prod", u0 + a, u1, 16)) for a in range(16)])
                ts(R("co", u0 // 16, u1 // 16), ob, float(C0), None, OP.add)
                due(scat(R("cb", 0, 2576), R("co", u0 // 16, u1 // 16), U("ab")), RL * t + DUE["pack"][u1 // 512])
        for o in range(N):
            ts(R("c16", 64 + 64 * o, 128 + 64 * o), R("cb", C0 + 1 + 512 * o, C0 + 65 + 512 * o), col(21), SH, OP.add, OP.min)
            if o == 0:
                mm([(R("p7", 0, 4), Z("zf", 1, a), R("c16", 64 + a, 128, 16)) for a in range(16)])
                ts(R("obz", 0, 4), R("p7", 0, 4), SH, None, OP.add)
                cp(R("eo", 0, 64), ("ind", TAB, R("obz", 0, 4)))
                cp(R("xbz", 0, 64), ("ind", XT, R("obz", 0, 4)))
        mm([(R("p3", 0, 16), Z("zf", 2, a), R("c16", 64 + a, 320, 16)) for a in range(16)])
        ts(R("obz", 16, 32), R("p3", 0, 16), SH, None, OP.add)
        cp(R("xbz", 256, 320), ("ind", XT, R("obz", 16, 20)))
        mm([(R("p7", 4, 16), Z("zf", 1, a), R("c16", 128 + a, 320, 16)) for a in range(16)])
        ts(R("obz", 4, 16), R("p7", 4, 16), SH, None, OP.add)
        cp(R("eo", 64, 256), ("ind", TAB, R("obz", 4, 16)))
        for o in (0, 256):
            for lo, hi in ((o + 64, o + 128), (o + 128, o + 256)):
                if lo - o < XV:
                    cp(R("xbz", lo, hi), ("ind", XT, R("obz", lo // 16, hi // 16)))
                else:
                    due(act(R("xbz", lo, hi), ("ind", XT, R("obz", lo // 16, hi // 16)), AF.Identity), RL * t + DUE["xbz"])
        ts(R("sbf", 0, 256), R("eo", 0, 256), -SH, None, OP.add)
        ts(R("nj", 0, 256), R("eo", 0, 256), float(W), None, OP.is_equal)
        for lo in (0, 128):
            mm([(R("p6", lo, lo + 128), M("I"), R("xbz", 256 + lo, 384 + lo)), (R("p6", lo, lo + 128), M("NI"), R("xbz", lo, lo + 128))])
            act(R("dzb", lo, lo + 128), R("p6", lo, lo + 128), AF.Abs)
        for a in range(16):
            dma("s", T.shf[a:128:16, 0:304], T.c16[5:128:16, 15 - a:319 - a], [R("c16", 15 - a, 319 - a)], [], "sf", 2500, eqs)
        landed(R("shf", 0, 304), "sf")
        mm([(R("p1", 0, 256), SEL(5), R("c16", 64, 320))])
        eqs = [tt(R("eq", 256 * q, 256 * q + 256), R("shf", 48 - 16 * q, 304 - 16 * q), R("p1", 0, 256), OP.is_equal) for q in range(4)]
        mm([(R("p1", 0, 256), M("BD"), R("eq", 256 * q, 256 * q + 256)) for q in range(4)])
        act(R("cnt", 0, 256), R("p1", 0, 256), AF.Identity)
        ts(R("bl", 0, 16), R("obz", 0, 16), -SH, None, OP.add)
        mm([(R("p1", 0, 16), IF, R("bl", 0, 16))] + [(R("p1", 0, 16), Z("zb", 0, a), R("cnt", a, 256, 16)) for a in range(16)])
        tt(R("tg", 0, 16), R("dw", 0, 16), R("p1", 0, 16), OP.min)
        if t < RO - 1:
            mm([(R("p1", 256 + 16 * s, 272 + 16 * s), blk("rep", s, 128), R("tg", 0, 16)) for s in range(N)])
            ts(R("mo", 0, 64), R("p1", 256, 320), SH, None, OP.add)
        else:
            s_o = send([(R("tg", 0, 16), blk("lt", rank, 16), peers)], "lt%d" % rank, off_eng)[0]
        due(len(ops) - 1, RL * t + DUE["mo"])
        sent = {}
        flip[2] = 0
        clock[0] = RL * t + DUE["max"]
        for c0, c1 in parts(SUB):
            due(act(R("xe", 16 * c0, 16 * c1), ("ind", XT, R("eo", c0, c1)), AF.Identity), RL * t + DUE["xe"])
        for h, (s0, s1) in enumerate(parts(JC[t])):
            n = s1 - s0
            H = lambda b, o=0: R(b, o + s0, o + s1)
            K = lambda b, k: R(b, 16 * s0 + k, 16 * s1, 16)
            hb = "p%d" % (4 + h % 2)
            r2, r1 = R(hb, 0, 128, 1, n), R(hb, 128, 256, 1, n)
            byv = [kp for kp in range(2) if (h, kp) not in ABS[t]]
            odd = lambda r, kp: R(r[0], r[1] + kp, r[2], 2, r[4])
            for c0, c1 in [(s0 + a, s0 + b) for a, b in (parts([64] * (n // 64)) if h == 0 else [(0, n)])]:
                st = (c1 - c0) // 32
                bb, bz = SPREAD[flip[2] % 2]
                flip[2] += 1
                mm([(R(bb, d, 512, 16 // st), M("I"), R("xbz", c0, c1)) for d in range(16 // st)])
                if byv:
                    mm([(R(bz, d, 512, 16 // st), M("I"), R("xbz", 256 + c0, 256 + c1)) for d in range(16 // st)])
                if c1 == s1:
                    mm([(r2, H("nj"), M("IB")), (r1, H("nj"), M("IB")), (r2, H("xbz"), M("BDH")), (r1, H("dzb"), M("NBDH"))] +
                       [(odd(r, kp), H("xbz", 256), odd(M("NBDH"), kp)) for kp in byv for r in (r1, r2)], True, False)
                    for kp in range(2):
                        o, w8 = (128, g8("NBDH")) if kp in byv else (0, g8("BDH"))
                        mm([(R(hb, o + k, o + 128, 16, n), K("xe", k), w8) for k in range(kp, 16, 2)], False, False)
                items = [(kp, eb) for kp in range(st) for eb in ("e2", "e1")]
                items = [x for x in items if x[1] == "e2" or x[0] % 2 in byv] + [x for x in items if x[1] == "e1" and x[0] % 2 not in byv]
                for kp, eb in items:
                    xs = R("xe", 16 * c0 + kp, 16 * c1, st)
                    tgt, hi, w8 = (bb, 128, g8("NBD")) if eb == "e2" else (bz, 256, R("b16", 0, 16))
                    if eb == "e1" and kp % 2 not in byv:
                        bank = SPREAD[flip[2] % 2][flip[3] % 2]
                        flip[3] += 1
                        mm([(R(bank, 0, 512), M("I"), xs)] +
                           [(R(bank, d, 512, 16 // st), M("NI"), R("xbz", 256 + c0, 256 + c1)) for d in range(16 // st)])
                        due(act(R(eb, xs[1], xs[2], st), R(bank, 0, 512), AF.Abs), clock[0] + DUE["abs"])
                        w8 = R("b16", 16, 32)
                    else:
                        chain(tt(R(eb, xs[1], xs[2], st), xs, R(tgt, 0, 512), OP.max))
                    if c1 == s1:
                        mm([(R(hb, k, hi, 16, n), K(eb, k), w8) for k in range(kp, 16, st)], False, (kp, eb) == items[-1])
            pu, px = R("p6", 0, n), R("p6", 128, 128 + n)
            mm([(pu, M("I4"), R("mhalf", 0, n)), (px, SEL(8), H("c16", 64)), (px, M("IB"), R("ones", 0, n)), (px, M("TR0"), H("nj"))], True, False)
            ev, rf = R("er", 2 * s0, 2 * s0 + n), R("er", 2 * s0 + n, 2 * s1)
            act(R("fl", 256 * h, 256 * h + 256, 1, n), R(hb, 0, 256, 1, n), AF.Sign)
            mm([(R(hb, 256 + n * i, 256 + n * i + n), R("fl", 256 * h + 128 * i, 256 * h + 128 * i + 128, 1, n), M("NI", n)) for i in range(2)])
            act(R("er", 2 * s0, 2 * s1), R(hb, 256, 256 + 2 * n), AF.Relu)
            mm([(pu, M("NBDB"), rf), (px, M("BDB"), rf), (pu, M("I4"), ev), (px, M("TR0"), ev)], False, True)
            tt(H("uu"), H("sbf"), pu, OP.max)
            due(tt(H("md"), H("uu"), px, OP.min), RL * t + DUE["md"][h if s1 < 256 else 2])
            if t < RO - 1:
                got = lambda s, k=1: R("mf32", 4 * s0 + n * s, 4 * s0 + n * (s + k))
                for bank, lo, hi in (("p1", 3, 4), ("p6", 2, 3), ("p1", 0, 2)) if s1 == 256 else (("p1", 0, 4),):
                    mm([(R(bank, n * s, n * s + n), blk("rep", s, 128), H("md")) for s in range(lo, hi)])
                    act(got(lo, hi - lo), R(bank, lo * n, hi * n), AF.Identity, SH)
                for s in range(N - 1, -1, -1):
                    due(scat(R("tab", 0, TW), R("mo", 16 * s + s0 // 16, 16 * s + s1 // 16), got(s)), RL * t + DUE["tab"][h])
            else:
                to = [j for j in range(s0 // 64, s1 // 64) if ring[j] != rank]
                if to:
                    out = send([(blk("md", j, 64), blk("lm", rank, 64), [T.cores[ring[j]]]) for j in to], "lm%d" % rank, off_eng)
                    sent.update({j: out for j in to})
        if t == RO - 2:
            for d in ring[:-1]:
                dma("s", ap(blk("stg", d)), T.tab[rows(0), V * d:V * d + V], [R("tab", V * d, V * d + V)], [blk("stg", d)], "sg%d" % d, 3000)
            s_y, ky = send([(blk("stg", d), blk("ls", rank), [T.cores[d]]) for d in ring[:-1]], "sy%d" % rank, off_eng)
            for s in ring[::-1]:
                if s == rank:
                    dma("s", T.yb[rows(s), 0:V], T.tab[rows(0), V * s:V * s + V], [R("tab", V * s, V * s + V)], [], "yb", 3000)
                else:
                    arrive(blk("ls", s), "sy%d" % s, ky, [s_y], 9000)
                    dma("s", T.yb[rows(s), 0:V], ap(blk("ls", s)), [blk("ls", s)], [], "yb", 3000)
            due(landed(R("yb", 0, V), "yb"), RL * (RO - 1) + DUE["test"] + 15000)
    terms = []
    for s in ring:
        j = 4 * ((rank - s - 1) % N)
        if s != rank:
            arrive(blk("lt", s, 16), "lt%d" % s, NE, [s_o], 3000)
        got = R("lt", 16 * s + j, 16 * s + j + 4) if s != rank else R("tg", j, j + 4)
        terms += [(R("p1", 256 + 4 * q, 260 + 4 * q), PQ(s, q), got) for q in range(N)]
    mm(terms)
    ts(R("mo", 0, 16), R("p1", 256, 272), SH - V * rank, None, OP.add)
    for s in ring[-2::-1] + [rank]:
        j = (rank - s - 1) % N
        if s != rank:
            arrive(blk("lm", s, 64), "lm%d" % s, sent[j][1], [sent[j][0]], 3500)
        got = blk("lm", s, 64) if s != rank else blk("md", j, 64)
        mm([(blk("p1", q, 64), PQ(s, q), got) for q in range(N)], j == 0, s == rank)
    act(R("mf32", 128, 256), R("p1", 128, 256), AF.Identity, SH)
    act(R("mf32", 0, 128), R("p1", 0, 128), AF.Identity, SH)
    for q in range(N - 1, -1, -1):
        scat(R("yb", 0, TW), blk("mo", q, 4), blk("mf32", q, 64))
    dma("a", T.y[:, 0:512], T.yb[:, 0:512], [R("yb", 0, 512)], [], "st0", 2500)
    dma("s", T.y[:, 512:V], T.yb[:, 512:V], [R("yb", 512, V)], [], "st1", 2500)
    return ops, Q, nloc[0]


def order(ops, kids, key):
    n = len(ops)
    left = [len(o["deps"]) for o in ops]
    rdy = [0.0] * n
    pool = {e: [] for e in "vapgsx"}
    free = {e: 0.0 for e in "vapgsx"}
    for i in range(n):
        if left[i] == 0:
            pool[ops[i]["eng"]].append(i)
    seq = []
    while len(seq) < n:
        t0, e = min((max(free[e], min([rdy[i] for i in p])), e) for e, p in pool.items() if p)
        i = min([i for i in pool[e] if rdy[i] <= t0 + LOOK], key=lambda i: key[i])
        pool[e].remove(i)
        t0 = max(t0, rdy[i])
        if e != "x":
            free[e] = t0 + ops[i]["cost"]
        done = t0 + ops[i]["cost"] + max(ops[i]["lat"], 0.0)
        seq.append(i)
        for k in kids[i]:
            rdy[k] = max(rdy[k], done + (HOP if ops[k]["deps"][i] else 0.0))
            left[k] -= 1
            if left[k] == 0:
                pool[ops[k]["eng"]].append(k)
    return seq


def span(ops, seq, pe, ga, hop):
    done = [0.0] * len(ops)
    free = {e: 0.0 for e in "vapgsx"}
    for i in seq:
        o = ops[i]
        t0 = max([free[o["eng"]]] + [done[j] + (hop if h else 0.0) for j, h in o["deps"].items()])
        c = o["cost"] * (pe if o["pe"] else 1.0) + CYC * (ga - GA) * o["ga"]
        if o["eng"] != "x":
            free[o["eng"]] = t0 + c
        done[i] = t0 + c + max(o["lat"], 0.0)
    return max(done)


FOUND = {}


def plan(ops):
    n = len(ops)
    kids = [[] for _ in range(n)]
    for i, o in enumerate(ops):
        for j in o["deps"]:
            kids[j].append(i)
    key = [0.0] * n
    for i in range(n - 1, -1, -1):
        key[i] = min([ops[i]["due"]] + [key[k] - HOP - ops[i]["cost"] - max(ops[i]["lat"], 0.0) for k in kids[i]])
    shifted = lambda shift: order(ops, kids, [k + shift.get(o["tag"], 0.0) for k, o in zip(key, ops)])
    if "shift" not in FOUND:
        score = lambda q: sum(span(ops, q, *f) for f in FIGS)
        rng = np.random.default_rng(1)
        tags = sorted(set(o["tag"] for o in ops if o["tag"] < 1000))
        shift = {}
        best = score(shifted(shift))
        for _ in range(TRIES):
            cand = dict(shift)
            for k in rng.choice(len(tags), int(rng.integers(1, 5))):
                cand[tags[int(k)]] = float(rng.normal()) * float(rng.choice([500.0, 2000.0, 8000.0]))
            val = score(shifted(cand))
            if val <= best:
                best, shift = val, cand
        FOUND["shift"] = shift
    return shifted(FOUND["shift"])


def emit(g, T, ops, Q, nloc):
    seq = plan(ops)
    need = set(j for o in ops for j, hard in o["deps"].items() if hard)
    count = {e: 0 for e in "vapg"}
    tok, seen = {}, {}
    for i in seq:
        o = ops[i]
        e = o["eng"]
        if e == "x":
            tok[i] = (o["sem"], o["val"])
            continue
        want = {}
        for j, hard in o["deps"].items():
            if hard and tok[j] is not None:
                want[tok[j][0]] = max(want.get(tok[j][0], 0), tok[j][1])
        for s, v in want.items():
            if seen.get((e, s), 0) < v:
                Q[e].wait_ge(T.sem[s], v)
                seen[(e, s)] = v
        ins = o["fn"]()
        if o["sem"] is not None:
            ins.then_inc(T.sem[o["sem"]], 16)
            tok[i] = (o["sem"], o["val"])
        elif o["lat"] < 0:
            tok[i] = None
        elif i in need:
            count[e] += 1
            ins.then_inc(T.sem["q" + e], 1)
            tok[i] = ("q" + e, count[e])
    for e in count:
        g.wait_ge(T.sem["q" + e], count[e])
    g.wait_ge(T.sem.loc, nloc)
    g.wait_ge(T.sem.st0, 16)
    g.wait_ge(T.sem.st1, 16)


def rank_program(g, core, T, topo):
    if T.rank_of(core) is not None:
        ops, Q, nloc = build(g, core, T, topo)
        emit(g, T, ops, Q, nloc)
